import numpy as np, ml_dtypes
CORES = [2,6,10,14,18,22,26,30]
N = 8
BF = ml_dtypes.bfloat16
def gentries(a):
    return np.ascontiguousarray(a.reshape(8, 16, -1).transpose(0, 2, 1)).reshape(8, -1)
def gtable(e):
    e = np.asarray(e); return np.ascontiguousarray(e.reshape(8, -1, 16).transpose(0, 2, 1)).reshape(128, -1).astype(np.int32)
W, K, RO, LG = 4096, 1, 3, 3
def turn(rng):
    o = np.argsort(rng.random((8, W)), axis=1); p = np.zeros((8, W), np.int64); h = W >> 1
    np.put_along_axis(p, o[:, :h], o[:, h:], 1); np.put_along_axis(p, o[:, h:], o[:, :h], 1)
    return p
def near(rng, p, noise):
    b = rng.integers(0, 256, (8, 16, W)); lo = np.minimum(np.arange(W)[None, :], p)
    b = np.take_along_axis(b, lo[:, None, :], 2)
    return np.clip(b[None] + rng.integers(-noise, noise + 1, (N, 8, 16, W)), 0, 255)
def pack(x, m):
    return {"fr": np.ascontiguousarray(x.reshape(N, 128, W)).astype(np.float32).astype(BF), "ptr": np.stack([gtable(a) for a in m])}
def setup_inputs(rng):
    p = turn(rng); x = near(rng, p, 6)
    x = np.where(rng.random((N, 8, 1, W)) < 0.25, rng.integers(0, 256, (N, 8, 16, W)), x)
    x = np.where(rng.random((8, 1, W)) < 0.06, rng.integers(0, 256, (8, 16, 1)), x)
    share = rng.choice(np.array([0.3, 0.5, 0.7]), (N, 8, 1))
    m = np.where(rng.random((N, 8, W)) < share, p[None], rng.integers(0, W, (N, 8, W)))
    return pack(x, m)
def setup_inputs_alike(rng):
    v = np.arange(W); h = (v + (W >> 1)) & (W - 1); x = near(rng, np.tile(h, (8, 1)), 5); m = np.zeros((N, 8, W), np.int64)
    for r in range(N):
        o = rng.permutation(8)
        for g in range(8):
            k = int(o[g])
            if k == 0:
                m[r, g] = 0; x[r ^ 1, g, :, 0] = 255; x[r ^ 1, g, :, 1] = 254
            elif k == 1: m[r, g] = W - 1
            elif k == 2: m[r, g] = v
            elif k == 3: m[r, g] = (v + 1) & (W - 1)
            elif k == 4: m[r, g] = W - 1 - v
            elif k == 5: m[r, g] = rng.choice(np.array([0, 3, W >> 1, W - 1]), W)
            else: m[r, g] = np.where(rng.random(W) < 0.7, h, rng.integers(0, W, W))
    return pack(x, m)
def setup_inputs_corners(rng):
    v = np.arange(W); L = W >> 5; low = np.arange(L); x = rng.integers(0, 256, (N, 8, 16, W)); m = np.zeros((N, 8, W), np.int64)
    role = np.zeros(N >> 1, np.int64); c0 = int(rng.integers(0, N >> 1)); role[c0 ^ 1] = 1; flip = int(rng.integers(0, 2))
    rest = [c for c in range(N >> 1) if c != c0 and c != c0 ^ 1]
    for i in range(len(rest)): role[rest[i]] = 2 + (i ^ flip)
    D = rng.integers(0, 32, 8); D[int(rng.integers(0, 8))] = 0; side = rng.integers(0, 2, 8); lone = int(rng.integers(0, 8))
    for c in range(N >> 1):
        k = int(role[c])
        for g in range(8):
            a = 2 * c + (int(side[g]) ^ int(k == 1)); b = a ^ 1
            if k == 2:
                m[a, g] = (v + g) & (W - 1); m[b, g] = (v + 1 + g) & (W - 1)
                x[a, g] = 255 * rng.integers(0, 2, (1, W))
                x[b, g] = np.where(rng.random((1, W)) < 0.5, 255 * rng.integers(0, 2, (1, W)), x[b, g])
                continue
            if k == 3 and g & 1 == 1:
                m[a, g] = 0; m[b, g] = W - 1 if g & 2 == 2 else v
                continue
            if k == 3: w = rng.permutation(W)
            else:
                kind = 1 if k == 1 and g == lone else int(rng.integers(0, 4))
                if kind == 0: lo = low
                elif kind == 1: lo = L - 1 - low
                elif kind == 2: lo = low ^ 1
                else: lo = np.argsort(rng.random((32, L)), axis=1)
                w = (((np.arange(32)[:, None] + int(D[g]) + 4 * int(k == 1)) & 31) * L + lo).reshape(-1)
            m[a, g] = w; m[b, g, w] = v
            x[b, g][:, w] = np.clip(x[a, g] + rng.integers(-7, 8, (16, W)), 0, 255)
            if k == 3: m[a, g] = np.where(rng.random(W) < 0.5, rng.integers(0, W, W), m[a, g])
            if k == 1 and g == lone:
                u = L * int(rng.integers(0, 32)) + int(rng.integers(2, L)); m[a, g, u] = int(w[u]) ^ 1
    return pack(x, m)
def setup_inputs_ends(rng):
    p = turn(rng); v = np.arange(W); lo = np.minimum(v[None, :], p)
    kind = rng.integers(0, 3, (8, 1, W)); b = 255 * np.where(kind == 2, rng.integers(0, 2, (8, 16, W)), kind)
    b = np.take_along_axis(b, lo[:, None, :], 2)
    x = np.where(rng.random((N, 8, 1, W)) < 0.25, 255 * rng.integers(0, 2, (N, 8, 16, W)), b[None])
    one = (rng.random((N, 8, 1, W)) < 0.25) & (np.arange(16)[:, None] == rng.integers(0, 16, (N, 8, 1, W)))
    x = np.where(one, np.abs(x - 1), x)
    u = rng.random((8, W)); hit = np.minimum(u, np.take_along_axis(u, p, 1)) < 0.15
    m = np.where(hit[None] & (rng.random((N, 8, W)) < 0.9), p[None], (W - 1) * rng.integers(0, 2, (N, 8, W)))
    for r in range(N):
        for g in range(8):
            s = (r ^ g) & 1
            if s == 1: m[r, g, 0] = W - 1; m[r, g, W - 1] = 0
            else: m[r, g, 0] = 0; m[r, g, W - 1] = W - 1
            m[r, g, W - 2] = W - 1
            for c in (0, 1, 2, 3, W - 2, W - 1): x[r, g, :, c] = 255 * s
            t = g >> 1
            if t > 0: x[r, g, int(rng.integers(0, 16)), (0, W - 1, 0, 1)[t]] = abs(255 * s - 1)
    return pack(x, m)
def setup_inputs_spread(rng):
    p = turn(rng); x = near(rng, p, 3); lo = np.minimum(np.arange(W)[None, :], p)
    sh = np.take_along_axis(rng.integers(0, 8, (8, W)), lo, 1)[None]
    sh = np.where(rng.random((N, 8, W)) < 0.3, rng.integers(0, 8, (N, 8, W)), sh)
    x = (x >> sh[:, :, None, :]) * (rng.random((N, 8, 1, W)) > 0.0625)
    w = np.minimum((W * rng.random((N, 8, W)) ** 4).astype(np.int64), W - 1)
    w = np.where(rng.random((N, 8, 1)) < 0.5, w, W - 1 - w)
    m = np.where(rng.random((N, 8, W)) < 0.4, p[None], w)
    return pack(x, m)
def setup_inputs_ties(rng):
    p = turn(rng); pal = rng.choice(np.array([0, 1, 100, 127, 128, 254, 255]), (8, 16, 4))
    pal[:, 0, 0] = 0; pal[:, 1, 0] = 200; pal[:, :, 1] = pal[:, :, 0]; pal[:, 0, 1] = 200; pal[:, 1, 1] = 0
    pal[:, 0:2, 2] = 128; pal[:, 0:2, 3] = 5
    ix = rng.integers(0, 4, (N, 8, W))
    x = np.take_along_axis(np.tile(pal[None], (N, 1, 1, 1)), ix[:, :, None, :], 3)
    x = np.where(rng.random((N, 8, 1, W)) < 0.125, rng.integers(0, 256, (N, 8, 16, W)), x)
    m = np.where(rng.random((N, 8, W)) < 0.5, p[None], rng.integers(0, W, (N, 8, W)))
    return pack(x, m)
def check_inputs(d):
    bad = []
    for k, lo, hi in (("fr", 0, 255), ("ptr", 0, W - 1)):
        a = np.asarray(d[k]).astype(np.float64)
        if not (np.min(a) >= lo and np.max(a) <= hi): bad.append("range of " + k)
        if not np.all(a == np.floor(a)): bad.append("whole numbers in " + k)
    return bad
def reference(fr, ptr):
    x = fr.astype(np.float32).astype(np.int32).reshape(N, 8, 16, W)
    m = np.stack([gentries(a) for a in ptr]).astype(np.int64)
    cnt = [0] * N; own = np.arange(W)[None, :]
    for t in range(RO):
        h = 1 << (t % LG); chosen = []
        for r in range(N):
            a, n, xq = m[r], m[r ^ h], x[r ^ h]
            es = [a]
            for i in range(K): es.append(np.take_along_axis(a, np.take_along_axis(n, es[-1], 1), 1))
            es.append((np.roll(a, 1, axis=1) + 1 + (cnt[r] & 3)) & (W - 1))
            far = np.stack([np.sum(np.abs(np.take_along_axis(xq, e[:, None, :], 2) - x[r]), axis=1) for e in es])
            first = np.argmin(far, axis=0)
            chosen.append(np.take_along_axis(np.stack(es), first[None], 0)[0])
        lifted = []
        for r in range(N):
            q = r ^ h
            con = np.take_along_axis(chosen[q], chosen[r], 1) == own
            c = con[:, None, :]; y = np.take_along_axis(x[q], chosen[r][:, None, :], 2)
            if r < q: lifted.append(np.where(c, (x[r] + y) >> 1, x[r]))
            else:
                z = np.abs(x[r] - y); lifted.append(np.where(c, z, z >> 1))
            cnt[r] = int(np.sum(con))
        x = np.stack(lifted); m = np.stack(chosen)
    return {"yf": x.reshape(N, 128, W).astype(np.float32).astype(BF), "yp": np.stack([gtable(a) for a in m]).astype(np.float32)}

@@ -1,0 +1,558 @@
+import numpy as np
+from concourse.bass import DstId, RemoteDMATransfer
+from concourse.mybir import AluOpType as ALU, ActivationFunctionType as ACT
+
+W = 4096
+RO = 3
+GC = 1024
+NG = W // GC
+CHOICE = [(0, 128), (128, 256)]
+XPATH = {(2, 0), (2, 1), (2, 2)}
+PW = 256
+NP = 256 // PW
+LIFT = [[0, 512, 1024, 2048, 3072, 4096], [0, 512, 1024, 2048, 3072, 4096], [0, 1024, 2048, 3072, 3584, 4096]]
+MAGIC = 12582912.0
+
+SCRATCH = {
+    "F0": ("sbuf", [128, 2 * W], "bfloat16"), "F1": ("sbuf", [128, 2 * W], "bfloat16"),
+    "F2": ("sbuf", [128, 2 * W], "bfloat16"), "F3": ("sbuf", [128, W], "bfloat16"),
+    "XP0": ("sbuf", [128, W + 16], "bfloat16"), "XP1": ("sbuf", [128, W + 16], "bfloat16"),
+    "XP2": ("sbuf", [128, W + 16], "bfloat16"),
+    "HZ": ("sbuf", [128, 2 * W], "bfloat16"), "A": ("sbuf", [128, 3 * W], "bfloat16"),
+    "D": ("sbuf", [128, W], "bfloat16"), "Y": ("sbuf", [128, W], "bfloat16"),
+    "Wn": ("sbuf", [128, W], "bfloat16"), "G1": ("sbuf", [128, W], "bfloat16"), "G2": ("sbuf", [128, W], "bfloat16"),
+    "ab": ("sbuf", [128, 4 * NP, 2, PW], "bfloat16"), "land": ("sbuf", [128, 6 * NP, 2, PW], "bfloat16"),
+    "kb": ("sbuf", [128, 256], "bfloat16"), "con": ("sbuf", [128, 256], "bfloat16"), "junk": ("sbuf", [128, 256], "bfloat16"),
+    "qi": ("sbuf", [128, 256], "int32"), "abi": ("sbuf", [128, 2, 256], "int32"), "ki": ("sbuf", [128, 256], "int32"),
+    "u16": ("sbuf", [128, 7 * 256], "uint16"),
+    "e0x": ("sbuf", [128, 264], "float32"), "dl2": ("sbuf", [128, 256], "float32"),
+    "tmp": ("sbuf", [128, 4 * 256], "float32"), "posv": ("sbuf", [128, 256], "float32"),
+    "cf": ("sbuf", [128, 256], "float32"), "cb": ("sbuf", [128, 256], "bfloat16"),
+    "ones": ("sbuf", [128, 512], "bfloat16"), "ones32": ("sbuf", [128, 128], "float32"),
+    "B": ("sbuf", [128, 4 * 144], "bfloat16"), "Id": ("sbuf", [128, 7 * 128], "bfloat16"),
+    "M32": ("sbuf", [128, 4 * 128], "float32"),
+    "col": ("sbuf", [128, 32], "float32"), "coli": ("sbuf", [128, 16], "int32"),
+    "Pd0": ("psum", [128, 512], "float32"), "Pd1": ("psum", [128, 512], "float32"),
+    "Px0": ("psum", [128, 512], "float32"), "Px1": ("psum", [128, 512], "float32"),
+    "Pw0": ("psum", [128, 512], "float32"), "Pw1": ("psum", [128, 512], "float32"),
+    "Pq": ("psum", [128, 512], "float32"), "Pm": ("psum", [128, 512], "float32"),
+}
+NDMA = 60
+SEMAPHORES = (["qV", "qS", "qP", "qG", "sent"] + ["lp%d" % i for i in range(12)] + ["fa%d" % i for i in range(RO)]
+              + ["dm%d" % i for i in range(NDMA)])
+
+CYC, GAM, FIX, PEC = 0.00104, 1.56, 0.06, 0.00052
+VBIAS, WINDOW, SEED, TRIES, MIX = 1.0, 0.1, 1, 1000, 0.5
+LAT_OTHER, LAT_SAME = 0.12, 0.05
+DMA_LAT, DMA_RATE, REM_ISSUE, REM_LAT, REM_RATE, ROW = 2.0, 20e3, 0.8, 2.2, 16e3, 0.03
+U_M, U_POS, U_SIG, U_PHI, U_P1, U_E1, U_E2 = [256 * i for i in range(7)]
+I_1, I_N1, I_H, I_NQ, I_256, I_16, I_4096 = [128 * i for i in range(7)]
+C_PM, C_PM256, C_W, C_WC, C_CS, C_CC, C_CC2 = 0, 1, 2, 12, 16, 20, 24
+
+
+def build(g, core, T, topo):
+    rank = T.rank_of(core)
+    ops = []
+    acc = {}
+    Q = {"V": g.vector, "S": g.scalar, "P": g.tensor, "G": g, "Y": g.sync, "A": g.scalar}
+
+    def add(name, alts, reads, writes, kind="c", extra=(), info=None):
+        k = len(ops)
+        deps = set(extra)
+        eng = list(alts)[0] if len(alts) == 1 else None
+        for lst, wr in ((reads, False), (writes, True)):
+            for (b, lo, hi) in lst:
+                ps = b[0] == "P" and b in SCRATCH and SCRATCH[b][0] == "psum"
+                for (j, l2, h2, w2, e2) in acc.get(b, []):
+                    if j == k:
+                        continue
+                    if (ps and e2 != eng) or ((wr or w2) and l2 < hi and lo < h2):
+                        deps.add(j)
+                acc.setdefault(b, []).append((k, lo, hi, wr, eng))
+        ops.append({"name": name, "alts": alts, "deps": deps, "kind": kind, "info": info})
+        return k
+
+    def ap(r):
+        if r[0] in ("ab", "land"):
+            if r[2] - r[1] == 2 * PW:
+                return T[r[0]][:, r[1] // (2 * PW), :, :]
+            return T[r[0]][:, r[1] // (2 * PW), r[1] // PW % 2, r[1] % PW:(r[2] - 1) % PW + 1]
+        if r[0] == "abi":
+            return T.abi[:, r[1] // 256, r[1] % 256:(r[2] - 1) % 256 + 1]
+        return T[r[0]][:, r[1]:r[2]]
+
+    def n_(r):
+        return r[2] - r[1]
+
+    def vcost(n, f=1.0):
+        return FIX + max(64, n * f) * CYC
+
+    def two(r):
+        return SCRATCH[r[0]][2] in ("bfloat16", "uint16") and SCRATCH[r[0]][0] == "sbuf"
+
+    def sc(s):
+        return ap(s) if isinstance(s, tuple) else s
+
+    def ts(o, i, s1, s2, op0, op1=None, also_s=None):
+        rd = [i] + [s for s in (s1, s2) if isinstance(s, tuple)]
+        if op1 is None:
+            f = lambda: g.vector.tensor_scalar(ap(o), ap(i), sc(s1), None, op0)
+        else:
+            f = lambda: g.vector.tensor_scalar(ap(o), ap(i), sc(s1), sc(s2), op0, op1)
+        alts = {"V": (vcost(n_(o), 0.5 if two(o) and two(i) else 1.0), f)}
+        if also_s is not None:
+            alts["S"] = (vcost(n_(o)), lambda: g.scalar.activation(ap(o), ap(i), ACT.Identity, bias=also_s[1], scale=also_s[0]))
+        return add("ts", alts, rd, [o])
+
+    def cp(o, i):
+        return add("cp", {"V": (vcost(n_(o), 0.5 if two(o) and two(i) else 1.0), lambda: g.vector.tensor_copy(ap(o), ap(i)))}, [i], [o])
+
+    def tt(o, i0, i1, op):
+        ps = SCRATCH[i0[0]][0] == "psum" or SCRATCH[i1[0]][0] == "psum"
+        return add("tt", {"V": (vcost(n_(o), 1.0 if ps else 2.0), lambda: g.vector.tensor_tensor(ap(o), ap(i0), ap(i1), op))}, [i0, i1], [o])
+
+    def act(o, i, func, bias=0.0, scale=1.0, accum=None):
+        rd = [i] + [s for s in (bias, scale) if isinstance(s, tuple)]
+        if accum is None:
+            f = lambda: g.scalar.activation(ap(o), ap(i), func, bias=sc(bias), scale=sc(scale))
+            return add("act", {"S": (vcost(n_(o)), f)}, rd, [o])
+        f = lambda: g.scalar.activation(ap(o), ap(i), func, bias=sc(bias), scale=sc(scale), accum_out=ap(accum))
+        return add("act", {"S": (vcost(n_(o)), f)}, rd, [o, accum])
+
+    def ms(o, val):
+        return add("ms", {"V": (vcost(n_(o), 0.5 if two(o) else 1.0), lambda: g.vector.memset(ap(o), val))}, [], [o])
+
+    def gather(o, win, off, engs="VS", bias=0.0, minus=None, rows=None, name="ga"):
+        cost = FIX + n_(o) * GAM * CYC
+        src = lambda: ap(win).indirect(ap(off))
+        alts = {}
+        rd = [off] + ([win] if rows is None else rows)
+        if minus is not None:
+            alts["V"] = (cost, lambda: g.vector.tensor_tensor(ap(o), src(), ap(minus), ALU.subtract))
+            rd.append(minus)
+        else:
+            if "V" in engs:
+                if bias == 0.0:
+                    alts["V"] = (cost, lambda: g.vector.tensor_copy(ap(o), src()))
+                else:
+                    alts["V"] = (cost, lambda: g.vector.tensor_scalar(ap(o), src(), bias, None, ALU.add))
+            if "S" in engs:
+                alts["S"] = (cost, lambda: g.scalar.activation(ap(o), src(), ACT.Identity, bias=bias, scale=1.0))
+        return add(name, alts, rd, [o])
+
+    def mm(o, terms, f32=False):
+        def f():
+            ins = None
+            for x, (l, r, c0, st) in enumerate(terms):
+                rhs = T[r[0]][:, r[1] + c0:r[2]:st] if st > 1 else ap(r)
+                ins = g.tensor.matmul(ap(o), ap(l), rhs, x == 0, x == len(terms) - 1)
+            return ins
+        cost = FIX + len(terms) * max(64, n_(o)) * PEC * (4 if f32 else 1)
+        rd = list({l for l, r, c0, st in terms}) + list({r for l, r, c0, st in terms})
+        return add("mm", {"P": (cost, f)}, rd, [o])
+
+    def wrap(o, b0, src):
+        return mm(o, [(("B", b0 + 15 - i, b0 + 143 - i), src, i, 16) for i in range(16)])
+
+    def gop(o, i, f, n):
+        return add("g", {"G": (0.17 + 2 * n * CYC, f)}, [i] if i else [], [o])
+
+    def sel(o, i, pat, cmp, base, cm):
+        return gop(o, i, lambda: g.affine_select(ap(o), ap(i), pat, cmp, 0.0, base, cm), n_(o))
+
+    def dma(oap, iap, reads, writes, nbytes, q="Y", rows=128):
+        return add("dma", {q: (0.1, lambda: Q[q].dma_start(oap(), iap()))}, reads, writes, kind="d",
+                   info=DMA_LAT + (nbytes / DMA_RATE + rows * ROW) / 16)
+
+    sent = [0]
+    last = [None]
+
+    def mask_of(lst):
+        return sum(1 << e for e in lst)
+
+    def send(src, dsts, nbytes):
+        def f():
+            if len(dsts) == 1:
+                c, r, s, e = dsts[0]
+                rid, pid, se = topo.addr(c)
+                return g.remote_dma(ap(r), ap(src), T.sem[s], T.sem.sent, pid, rid, mask_of(e))
+            trs = []
+            for c, r, s, e in dsts:
+                rid, pid, se = topo.addr(c)
+                trs.append(RemoteDMATransfer(dst_ids=[DstId(rid=rid, pnc=pid)], dma_engine_mask=mask_of(e),
+                                             remote_sem=T.sem[s], src=ap(src), dst=ap(r)))
+            return g.remote_dma_fused(trs, local_sem=T.sem.sent)
+        sent[0] += sum(len(d[3]) for d in dsts)
+        k = add("send", {"G": (REM_ISSUE, f)}, [src], [], kind="r",
+                info=(nbytes / REM_RATE + 128 * ROW) / min(len(d[3]) for d in dsts))
+        ops[k]["after"] = last[0]
+        last[0] = k
+        return k
+
+    def arrive(sem, count, sends, rng):
+        return add("arr", {"X": (0.0, None)}, [], [rng], kind="a", extra=sends, info=(sem, count))
+
+    partner = [T.cores[rank ^ (1 << t)] for t in range(RO)]
+
+    def col(c):
+        return ("col", c, c + 1)
+
+    def ident(c):
+        return ("Id", c, c + 128)
+
+    dma(lambda: T.qi[:, :], lambda: T.ptr[:, :], [], [("qi", 0, 256)], 131072, q="A")
+    for j in range(NG):
+        dma(lambda j=j: T.F0[:, j * GC:(j + 1) * GC], lambda j=j: T.fr[:, j * GC:(j + 1) * GC], [],
+            [("F0", j * GC, (j + 1) * GC)], 256 * GC)
+    wrows = [("Wn%d" % r, 0, W) for r in range(7)]
+    add("ms", {"V": (vcost(W, 0.5), lambda: g.vector.memset(T.Wn[:], 1.0))}, [], wrows)
+    ms(("ones", 0, 512), 1.0)
+    ms(("ones32", 0, 128), 1.0)
+    gop(("coli", 0, 1), None, lambda: g.iota(T.coli[:, 0:1], [[0, 1]], 0, 1), 1)
+    gop(("cf", 0, 256), None, lambda: g.iota(T.cf[:, :], [[1, 256]], 0, 0, allow_small_or_imprecise_dtypes=True), 256)
+    sel(ident(I_1), ("ones", 0, 128), [[-1, 128]], ALU.is_equal, 0, 1)
+    B0 = ("B", 0, 144)
+    sel(B0, ("ones", 0, 144), [[0, 9], [1, 16]], ALU.is_equal, -15, 0)
+    sel(B0, B0, [[1, 144]], ALU.is_ge, 0, -1)
+    sel(B0, B0, [[-1, 144]], ALU.is_ge, 15, 1)
+    SH, WR, SHI, I32 = [("M32", 128 * i, 128 * i + 128) for i in range(4)]
+    sel(SH, ("ones32", 0, 128), [[1, 128]], ALU.is_equal, -1, -1)
+    sel(SH, SH, [[0, 8], [1, 16]], ALU.not_equal, 0, 0)
+    sel(WR, ("ones32", 0, 128), [[1, 128]], ALU.is_equal, 15, -1)
+    sel(WR, WR, [[0, 8], [1, 16]], ALU.is_equal, 0, 0)
+    tt(SHI, SH, ident(I_1), ALU.subtract)
+    for c, s in ((I_N1, -1.0), (I_H, 0.5), (I_NQ, -0.25), (I_256, 256.0), (I_16, 16.0), (I_4096, 4096.0)):
+        ts(ident(c), ident(I_1), s, None, ALU.mult, also_s=(s, 0.0))
+    ts(("coli", 4, 5), ("coli", 0, 1), 15, None, ALU.bitwise_and)
+    cp(col(C_PM), ("coli", 4, 5))
+    ts(col(C_PM256), col(C_PM), 256.0, None, ALU.mult)
+    ts(("posv", 0, 256), ("cf", 0, 256), col(C_PM256), None, ALU.add)
+    cp(("cb", 0, 256), ("cf", 0, 256))
+    for r, w in enumerate((256.0, 1.0, 256.0, 1.0, 1.0, 16.0, 8192.0)):
+        ts(col(C_W + r), col(C_PM), float(r), w, ALU.is_equal, ALU.mult)
+    tt(col(C_WC), col(C_W), col(C_W + 1), ALU.add)
+    tt(col(C_WC + 1), col(C_W + 2), col(C_W + 3), ALU.add)
+    tt(col(C_WC + 3), col(C_W + 4), col(C_W + 5), ALU.add)
+    tt(col(C_WC + 2), col(C_WC + 3), col(C_W + 6), ALU.add)
+    for x in range(3):
+        act(("B", 144 * (x + 1), 144 * (x + 2)), B0, ACT.Identity, scale=col(C_WC + x))
+    B_CL, B_G1, B_G2 = 144, 288, 432
+
+    def send_frame(t, x0, x1):
+        e = topo.engines(core, partner[t])
+        return send(("F%d" % t, x0, x1), [(partner[t], ("XP%d" % t, x0, x1), "fa%d" % t, e)], 256 * (x1 - x0))
+
+    def frame_arrives(t, sends):
+        arrive("fa%d" % t, len(sends) * len(topo.engines(partner[t], core)), sends, ("XP%d" % t, 0, W))
+        act(("XP%d" % t, W, W + 16), ("XP%d" % t, 0, 16), ACT.Identity)
+
+    def digits(s, c0, c1, high, bank):
+        a0 = 512 * s + PW * (c0 // PW)
+        w = c1 - c0
+        ai, bi = ("abi", c0, c1), ("abi", 256 + c0, 256 + c1)
+        ts(ai, ("qi", c0, c1), 15, None, ALU.bitwise_and)
+        ts(bi, ("qi", c0, c1), 4, 255, ALU.arith_shift_right, ALU.bitwise_and)
+        a, b = ("ab", a0 + c0, a0 + c1), ("ab", a0 + PW + c0, a0 + PW + c1)
+        add("cp", {"V": (vcost(2 * w), lambda: g.vector.tensor_copy(
+            T.ab[:, NP * s + c0 // PW, :, c0 % PW:c0 % PW + w], T.abi[:, :, c0:c1]))}, [ai, bi], [a, b])
+        if high:
+            ts(("ki", c0, c1), ("qi", c0, c1), 13, None, ALU.arith_shift_right)
+            cp(("kb", c0, c1), ("ki", c0, c1))
+            pb = (bank, c0, c1)
+            mm(pb, [(ident(I_4096), ("kb", c0, c1), 0, 1), (ident(I_16), ("cb", c0, c1), 0, 1)])
+            ts(("u16", U_SIG + c0, U_SIG + c1), pb, col(C_PM), None, ALU.add)
+        mm(("Pm", 2 * c0, 2 * c0 + w), [(ident(I_1), a, 0, 1), (ident(I_16), b, 0, 1)])
+        mm(("Pm", 2 * c0 + w, 2 * c1), [(ident(I_256), a, 0, 1), (ident(I_1), b, 0, 1)])
+        cp(("u16", U_M + 2 * c0, U_M + 2 * c1), ("Pm", 2 * c0, 2 * c1))
+        act(("e0x", 8 + c0, 8 + c1), ("Pm", 2 * c0, 2 * c0 + w), ACT.Identity)
+        if c1 == 256 and s < RO:
+            act(("e0x", 7, 8), ("Pm", 2 * c0 + w - 1, 2 * c0 + w), ACT.Identity)
+
+    def u_m(o0, o1, pos=0):
+        c0, c1 = [c for c in CHOICE if c[0] <= o0 < c[1]][0]
+        x = U_M + c0 + pos * (c1 - c0)
+        return ("u16", x + o0, x + o1)
+
+    def rows(buf, sl, p, r):
+        for x in range(2):
+            if p == NP - 1:
+                dma(lambda x=x: T.Wn[r + x::16, :], lambda x=x: T[buf][:, NP * sl:NP * sl + NP, x, :],
+                    [(buf, 512 * sl, 512 * sl + 512)], [wrows[r + x]], 65536, rows=128 * NP)
+
+    def engines_for(src, s):
+        r = T.rank_of(src)
+        to = [T.cores[r ^ (1 << t)] for t in (s - 1, s) if 0 <= t < RO]
+        es = [topo.engines(src, c) for c in to]
+        if len(es) == 1:
+            return [es[0][-8:]]
+        only = [e for e in es[0] if e not in es[1]]
+        if only:
+            return [only, es[1]]
+        h = len(es[0]) // 2
+        return [es[0][:h], es[1][h:]]
+
+    def exchange(s, p):
+        ts_ = [t for t in (s - 1, s) if 0 <= t < RO]
+        slot = {t: 2 * s - 1 + (t - (s - 1)) for t in ts_}
+        es = engines_for(core, s)
+        where = {t: ("land", 512 * slot[t] + 2 * PW * p, 512 * slot[t] + 2 * PW * (p + 1)) for t in ts_}
+        k = send(("ab", 512 * s + 2 * PW * p, 512 * s + 2 * PW * (p + 1)),
+                 [(partner[t], where[t], "lp%d" % (2 * slot[t] + p), es[x]) for x, t in enumerate(ts_)], 512 * PW)
+        for x, t in enumerate(ts_):
+            arrive("lp%d" % (2 * slot[t] + p), len(engines_for(partner[t], s)[x]), [k], where[t])
+        if s < RO:
+            rows("ab", s, p, 4)
+        for x, t in enumerate(ts_):
+            rows("land", slot[t], p, 0 if t == s - 1 else 2)
+
+    def chain(j):
+        c0, c1 = j * GC // 16, (j + 1) * GC // 16
+        pb = ("Pw%d" % (j & 1), 256 + c0, 256 + c1)
+        wrap(pb, B_G1, ("G1", j * GC, (j + 1) * GC))
+        cp(("u16", U_P1 + c0, U_P1 + c1), pb)
+
+    def chain2(j):
+        c0, c1 = j * GC // 16, (j + 1) * GC // 16
+        gather(("G2", j * GC, (j + 1) * GC), ("Wn", 0, W), ("u16", U_P1 + c0, U_P1 + c1), rows=wrows, name="G2")
+        wrap(("Pq", c0, c1), B_G2, ("G2", j * GC, (j + 1) * GC))
+        ts(("u16", U_E1 + c0, U_E1 + c1), ("Pq", c0, c1), -8192.0, None, ALU.add)
+
+    def last_candidate(t):
+        for pb, m0 in ((("Px0", 0, 256), SH), (("Px1", 0, 256), SHI)):
+            mm(pb, [(m0, ("e0x", 8, 264), 0, 1), (WR, ("e0x", 7, 263), 0, 1)], f32=True)
+        ts(("u16", U_E2, U_E2 + 256), ("Px0", 0, 256), col(C_CC) if t else 1.0, None, ALU.add)
+        act(("dl2", 0, 256), ("Px1", 0, 256), ACT.Identity, bias=col(C_CC2) if t else 16385.0)
+
+    def ptr_gather(x0, x1):
+        gather(("G1", x0, x1), ("Wn", 0, W), u_m(x0 // 16, x1 // 16, 1), rows=wrows, name="G1")
+
+    for c0, c1 in CHOICE:
+        digits(0, c0, c1, False, None)
+        if c1 % PW == 0:
+            exchange(0, c1 // PW - 1)
+    frame_arrives(0, [send_frame(0, j * GC, (j + 1) * GC) for j in range(NG)])
+    last_candidate(0)
+    for j in range(NG):
+        ptr_gather(j * GC, (j + 1) * GC)
+        chain(j)
+    for j in range(NG):
+        chain2(j)
+
+    slot = [0, 0]
+    for t in range(RO):
+        high = rank > (rank ^ (1 << t))
+        F, XP, FN = "F%d" % t, "XP%d" % t, "F%d" % (t + 1)
+        win = (XP, 0, W + 16)
+        done = 0
+        for ci, (c0, c1) in enumerate(CHOICE):
+            pd, pw = "Pd%d" % (ci & 1), "Pw%d" % (ci & 1)
+            w = c1 - c0
+            for j in range(c0 * 16 // GC, c1 * 16 // GC):
+                x0, x1, o0 = j * GC, (j + 1) * GC, j * GC // 16
+                for k, u in ((2, U_E2), (0, U_M), (1, U_E1)):
+                    off = ("u16", u + o0, u + o0 + GC // 16) if k else u_m(o0, o0 + GC // 16)
+                    if (k, j) in XPATH:
+                        gather(("Y", x0, x1), win, off, engs="S", name="Yx")
+                        for p in range(x0, x1, 512):
+                            px = ("Px%d" % (slot[0] & 1), 0, 512)
+                            slot[0] += 1
+                            mm(px, [(ident(I_1), ("Y", p, p + 512), 0, 1), (ident(I_N1), (F, p, p + 512), 0, 1)])
+                            act(("A", k * W + p, k * W + p + 512), px, ACT.Abs)
+                    else:
+                        d = ("D", (slot[1] % NG) * GC, (slot[1] % NG + 1) * GC)
+                        slot[1] += 1
+                        gather(d, win, off, minus=(F, x0, x1), name="D")
+                        act(("A", k * W + x0, k * W + x1), d, ACT.Abs)
+                    y0 = (0, 256, 256)[k] + o0 - c0
+                    wrap((pw if k == 1 else pd, y0, y0 + GC // 16), 0, ("A", k * W + x0, k * W + x1))
+            d0, d1, d2, ps = (pd, 0, w), (pw, 256, 256 + w), (pd, 256, 256 + w), (pw, 384, 384 + w)
+            t0, t1, t2, t3 = [("tmp", 256 * k + c0, 256 * k + c1) for k in range(4)]
+            ts(t0, d0, -1.0, None, ALU.add)
+            tt(d0, d2, t0, ALU.is_le)
+            tt(t1, d2, t0, ALU.min)
+            tt(d2, d0, ("dl2", c0, c1), ALU.mult)
+            tt(t2, d2, ("e0x", 8 + c0, 8 + c1), ALU.add)
+            tt(t3, ("Pq", c0, c1), t2, ALU.subtract)
+            tt(ps, d1, t1, ALU.is_le)
+            tt(d1, ps, t3, ALU.mult)
+            tt(("qi", c0, c1), d1, t2, ALU.add)
+            digits(t + 1, c0, c1, high, pw)
+            if c1 % PW == 0:
+                exchange(t + 1, c1 // PW - 1)
+        if t == RO - 1:
+            dma(lambda: T.yp[:, :], lambda: T.e0x[:, 8:264], [("e0x", 8, 264)], [], 131072)
+        for j in range(NG):
+            x0, x1, o0 = j * GC, (j + 1) * GC, j * GC // 16
+            if high:
+                z = ("HZ", W + x0, W + x1)
+                gather(z, ("A", 0, 3 * W), ("u16", U_SIG + o0, U_SIG + o0 + GC // 16), bias=-256.0, name="Z")
+                ts(("HZ", x0, x1), z, 0.5, -128.25, ALU.mult, ALU.add, also_s=(0.5, -128.25))
+            else:
+                gather(("Y", x0, x1), win, u_m(o0, o0 + GC // 16), name="Y")
+                for p in range(x0, x1, 512):
+                    px = ("Px%d" % (slot[0] & 1), 0, 512)
+                    slot[0] += 1
+                    mm(px, [(ident(I_H), ("Y", p, p + 512), 0, 1), (ident(I_H), (F, p, p + 512), 0, 1),
+                            (ident(I_NQ), ("ones", 0, 512), 0, 1)])
+                    ts((F, W + p, W + p + 512), px, MAGIC, -MAGIC, ALU.add, ALU.add)
+        sends = []
+        for j in range(len(LIFT[t]) - 1):
+            x0, x1 = LIFT[t][j], LIFT[t][j + 1]
+            c0, c1 = x0 // 16, x1 // 16
+            ptr_gather(x0, x1)
+            pb = ("Pw%d" % (j & 1), c0, c1)
+            wrap(pb, B_CL, ("G1", x0, x1))
+            tt(("con", c0, c1), pb, ("posv", c0, c1), ALU.is_equal)
+            pf = ("Pd%d" % (j & 1), c0, c1)
+            mm(pf, [(ident(I_4096), ("con", c0, c1), 0, 1), (ident(I_16), ("cb", c0, c1), 0, 1)])
+            phi = ("u16", U_PHI + c0, U_PHI + c1)
+            ts(phi, pf, col(C_PM), None, ALU.add)
+            if high:
+                gather((FN, x0, x1), ("HZ", 0, 2 * W), phi, bias=256.0, name="fin")
+            else:
+                gather((FN, x0, x1), (F, 0, 2 * W), phi, name="fin")
+            if t + 1 < RO:
+                sends.append(send_frame(t + 1, x0, x1))
+            else:
+                dma(lambda x0=x0, x1=x1: T.yf[:, x0:x1], lambda x0=x0, x1=x1: T.F3[:, x0:x1], [(FN, x0, x1)], [], 256 * (x1 - x0))
+        if t + 1 < RO:
+            for j in range(NG):
+                chain(j)
+            act(("junk", 0, 256), ("con", 0, 256), ACT.Identity, accum=col(C_CS))
+            mm(("Px0", 0, 1), [(("ones32", 0, 128), col(C_CS), 0, 1)], f32=True)
+            cp(("coli", 8, 9), ("Px0", 0, 1))
+            ts(("coli", 12, 13), ("coli", 8, 9), 3, None, ALU.bitwise_and)
+            ts(col(C_CC), ("coli", 12, 13), 1.0, None, ALU.add)
+            ts(col(C_CC2), ("coli", 12, 13), 16385.0, None, ALU.add)
+            last_candidate(t + 1)
+            for j in range(NG):
+                chain2(j)
+            frame_arrives(t + 1, sends)
+    return ops, Q, sent[0]
+
+
+def schedule(ops):
+    n = len(ops)
+    succ = [[] for _ in range(n)]
+    nxt = {}
+    for k, o in enumerate(ops):
+        for d in o["deps"]:
+            succ[d].append(k)
+        if o.get("after") is not None:
+            nxt[o["after"]] = k
+    base = [0.0] * n
+    for k in range(n - 1, -1, -1):
+        o = ops[k]
+        own = min(c for c, f in o["alts"].values())
+        if o["kind"] == "d":
+            own += o["info"]
+        if o["kind"] == "r":
+            own += REM_LAT + o["info"]
+        base[k] = own + LAT_OTHER + max([base[s] for s in succ[k]] + [0.0])
+        if k in nxt:
+            base[k] = max(base[k], o["info"] + base[nxt[k]])
+    alts = [[(e, "S" if e == "A" else e, c) for e, (c, f) in o["alts"].items()] for o in ops]
+    either = [k for k in range(n) if len(alts[k]) > 1]
+
+    def plan(prio, bias):
+        free = {"V": 0.0, "S": 0.0, "P": 0.0, "G": 0.0, "Y": 0.0, "X": 0.0, "link": 0.0, "dma": 0.0}
+        left = [len(o["deps"]) for o in ops]
+        end, eng, start = [0.0] * n, [None] * n, [0.0] * n
+        rdy = [[0.0] * len(a) for a in alts]
+        ready = [k for k in range(n) if left[k] == 0]
+        order = []
+        while ready:
+            cands = []
+            t0 = 1e9
+            for k in ready:
+                best = None
+                for x, (e, qn, c) in enumerate(alts[k]):
+                    s = max(free[qn], rdy[k][x])
+                    fin = s + c + (bias[k] if e == "V" else 0.0)
+                    if best is None or fin < best[3]:
+                        best = (s, e, c, fin, qn, k)
+                cands.append(best)
+                if best[0] < t0:
+                    t0 = best[0]
+            s, e, c, fin, qn, k = max((x for x in cands if x[0] <= t0 + WINDOW), key=lambda x: (prio[x[5]], -x[5]))
+            o = ops[k]
+            start[k], eng[k] = s, e
+            if e != "X":
+                free[qn] = s + c
+            end[k] = s + c
+            if o["kind"] == "d":
+                free["dma"] = max(free["dma"], s + c + DMA_LAT) + o["info"] - DMA_LAT
+                end[k] = free["dma"]
+            if o["kind"] == "r":
+                free["link"] = max(free["link"], s + c + REM_LAT) + o["info"]
+                end[k] = free["link"]
+            order.append(k)
+            ready.remove(k)
+            for x in succ[k]:
+                for y, a in enumerate(alts[x]):
+                    v = end[k] + (LAT_SAME if a[0] == e else LAT_OTHER)
+                    if v > rdy[x][y]:
+                        rdy[x][y] = v
+                left[x] -= 1
+                if left[x] == 0:
+                    ready.append(x)
+        return max(end), order, eng, start, end
+
+    rng = np.random.default_rng(SEED)
+    prio, bias = [MIX * base[k] - (1.0 - MIX) * k * base[0] / n for k in range(n)], [VBIAS] * n
+    best = plan(prio, bias)
+    for it in range(TRIES):
+        p2, b2 = list(prio), list(bias)
+        for _ in range(2):
+            k0 = int(rng.integers(0, n))
+            dv = float(rng.normal()) * 3.0
+            for k in range(k0, min(n, k0 + int(rng.integers(1, 12)))):
+                p2[k] += dv
+            b2[either[int(rng.integers(0, len(either)))]] = float(rng.choice([-2.0, 0.0, 1.0, 3.0]))
+        cand = plan(p2, b2)
+        if cand[0] <= best[0]:
+            best, prio, bias = cand, p2, b2
+    return best[1:]
+
+
+def rank_program(g, core, T, topo):
+    if T.rank_of(core) is None:
+        return
+    ops, Q, sent = build(g, core, T, topo)
+    order, eng, start, end = schedule(ops)
+    token = {}
+    count = {"V": 0, "S": 0, "P": 0, "G": 0}
+    seen = {}
+    top = {}
+    nd = 0
+    for k in order:
+        o, e = ops[k], eng[k]
+        if o["kind"] == "a":
+            token[k] = o["info"]
+            continue
+        qn = "S" if e == "A" else e
+        need = {}
+        for d in o["deps"]:
+            if e == "P" and eng[d] == "P":
+                continue
+            s, c = token[d]
+            need[s] = max(need.get(s, 0), c)
+        for s in sorted(need):
+            if seen.get((qn, s), 0) < need[s]:
+                Q[e].wait_ge(T.sem[s], need[s])
+                seen[(qn, s)] = need[s]
+        ins = o["alts"][e][1]()
+        if o["kind"] == "c":
+            count[e] += 1
+            token[k] = ("q" + e, count[e])
+            ins.then_inc(T.sem["q" + e], 1)
+        elif o["kind"] == "d":
+            token[k] = ("dm%d" % nd, 16)
+            nd += 1
+            ins.then_inc(T.sem[token[k][0]], 16)
+        if k in token:
+            top[token[k][0]] = token[k][1]
+    top["sent"] = sent
+    for s in sorted(top, key=lambda s: (s[0] == "d", len(s), s)):
+        if max([v for (qn, s2), v in seen.items() if s2 == s] + [0]) < top[s]:
+            g.wait_ge(T.sem[s], top[s])

@@ -1,53 +1,61 @@
-import numpy as np
 from concourse.bass import DstId, RemoteDMATransfer
 from concourse.mybir import AluOpType as ALU, ActivationFunctionType as ACT
 
 W = 4096
 RO = 3
+LW = W // 16
 GC = 1024
-NG = W // GC
-CHOICE = [(0, 128), (128, 256)]
-XPATH = {(2, 0), (2, 1), (2, 2)}
-PW = 256
-NP = 256 // PW
-LIFT = [[0, 512, 1024, 2048, 3072, 4096], [0, 512, 1024, 2048, 3072, 4096], [0, 1024, 2048, 3072, 3584, 4096]]
+LOAD = [0, 512, 1536, 2816, 4096]
+CAND = 2 * [[0, 1024, 2048, 3072, 4096]] + [[0, 1024, 2048, 3072, 3584, 4096]]
+XPATH = [{(0, 1), (2, 0), (2, 2)}] + 2 * [{(0, 0), (1, 1)}]
+CHOICE = [(0, 192), (192, 256)]
+EARLY = 1024
+TELL = 0
+LIFT = (2 * [[(1024, 2048), (2048, 3072), (3072, 4096), (0, 512), (512, 1024)]]
+        + [[(0, 1024), (1024, 2048), (2048, 3072), (3072, 3584), (3584, 4096)]])
 MAGIC = 12582912.0
+OFF = 255.0 * 65536
 
 SCRATCH = {
     "F0": ("sbuf", [128, 2 * W], "bfloat16"), "F1": ("sbuf", [128, 2 * W], "bfloat16"),
     "F2": ("sbuf", [128, 2 * W], "bfloat16"), "F3": ("sbuf", [128, W], "bfloat16"),
     "XP0": ("sbuf", [128, W + 16], "bfloat16"), "XP1": ("sbuf", [128, W + 16], "bfloat16"),
     "XP2": ("sbuf", [128, W + 16], "bfloat16"),
-    "HZ": ("sbuf", [128, 2 * W], "bfloat16"), "A": ("sbuf", [128, 3 * W], "bfloat16"),
-    "D": ("sbuf", [128, W], "bfloat16"), "Y": ("sbuf", [128, W], "bfloat16"),
+    "A": ("sbuf", [128, 3 * W], "bfloat16"), "H": ("sbuf", [128, W], "bfloat16"),
+    "Y0": ("sbuf", [128, W], "bfloat16"), "Y1": ("sbuf", [128, W], "bfloat16"), "Y2": ("sbuf", [128, W], "bfloat16"),
+    "EP": ("sbuf", [128, 4 * EARLY], "bfloat16"), "HP": ("sbuf", [128, EARLY], "bfloat16"),
+    "con": ("sbuf", [128, RO * 512], "bfloat16"), "lc": ("sbuf", [128, 512], "bfloat16"),
     "Wn": ("sbuf", [128, W], "bfloat16"), "G1": ("sbuf", [128, W], "bfloat16"), "G2": ("sbuf", [128, W], "bfloat16"),
-    "ab": ("sbuf", [128, 4 * NP, 2, PW], "bfloat16"), "land": ("sbuf", [128, 6 * NP, 2, PW], "bfloat16"),
-    "kb": ("sbuf", [128, 256], "bfloat16"), "con": ("sbuf", [128, 256], "bfloat16"), "junk": ("sbuf", [128, 256], "bfloat16"),
-    "qi": ("sbuf", [128, 256], "int32"), "abi": ("sbuf", [128, 2, 256], "int32"), "ki": ("sbuf", [128, 256], "int32"),
-    "u16": ("sbuf", [128, 7 * 256], "uint16"),
-    "e0x": ("sbuf", [128, 264], "float32"), "dl2": ("sbuf", [128, 256], "float32"),
-    "tmp": ("sbuf", [128, 4 * 256], "float32"), "posv": ("sbuf", [128, 256], "float32"),
-    "cf": ("sbuf", [128, 256], "float32"), "cb": ("sbuf", [128, 256], "bfloat16"),
-    "ones": ("sbuf", [128, 512], "bfloat16"), "ones32": ("sbuf", [128, 128], "float32"),
-    "B": ("sbuf", [128, 4 * 144], "bfloat16"), "Id": ("sbuf", [128, 7 * 128], "bfloat16"),
-    "M32": ("sbuf", [128, 4 * 128], "float32"),
+    "ab": ("sbuf", [128, 8, LW], "bfloat16"), "land": ("sbuf", [128, 10, LW], "bfloat16"),
+    "lu": ("sbuf", [128, 3 * LW], "uint16"), "u16": ("sbuf", [128, 9 * LW], "uint16"),
+    "qi": ("sbuf", [128, LW], "int32"), "wi": ("sbuf", [128, 2 * LW], "int32"), "abi": ("sbuf", [128, 2, LW], "int32"),
+    "lb": ("sbuf", [128, 5 * LW], "bfloat16"), "lf": ("sbuf", [128, 3 * LW], "float32"),
+    "row": ("sbuf", [128, LW], "float32"), "blk": ("sbuf", [128, 128], "float32"), "cb": ("sbuf", [128, LW], "bfloat16"),
+    "cc": ("sbuf", [128, LW], "bfloat16"), "ones": ("sbuf", [128, LW], "bfloat16"),
+    "ones32": ("sbuf", [128, 128], "float32"), "I32": ("sbuf", [128, 128], "float32"),
+    "B": ("sbuf", [128, 4 * 144], "bfloat16"), "Id": ("sbuf", [128, 15 * 128], "bfloat16"),
+    "BB": ("sbuf", [128, 8 * 128], "bfloat16"), "Hf": ("sbuf", [128, 128], "float16"),
     "col": ("sbuf", [128, 32], "float32"), "coli": ("sbuf", [128, 16], "int32"),
-    "Pd0": ("psum", [128, 512], "float32"), "Pd1": ("psum", [128, 512], "float32"),
-    "Px0": ("psum", [128, 512], "float32"), "Px1": ("psum", [128, 512], "float32"),
-    "Pw0": ("psum", [128, 512], "float32"), "Pw1": ("psum", [128, 512], "float32"),
-    "Pq": ("psum", [128, 512], "float32"), "Pm": ("psum", [128, 512], "float32"),
+    "PKa": ("psum", [128, 512], "float32"), "PKb": ("psum", [128, 512], "float32"),
+    "PM": ("psum", [128, 512], "float32"), "PQ": ("psum", [128, 512], "float32"), "PE": ("psum", [128, 512], "float32"),
+    "Px0": ("psum", [128, 512], "float32"), "Px1": ("psum", [128, 512], "float32"), "Px2": ("psum", [128, 512], "float32"),
 }
-NDMA = 60
-SEMAPHORES = (["qV", "qS", "qP", "qG", "sent"] + ["lp%d" % i for i in range(12)] + ["fa%d" % i for i in range(RO)]
-              + ["dm%d" % i for i in range(NDMA)])
+SEMAPHORES = (["qV", "qS", "qP", "qG", "sent"] + ["lp%d" % i for i in range(6)] + ["fa%d" % i for i in range(24)]
+              + ["dm%d" % i for i in range(12)])
 
-CYC, GAM, FIX, PEC = 0.00104, 1.56, 0.06, 0.00052
-VBIAS, WINDOW, SEED, TRIES, MIX = 1.0, 0.1, 1, 1000, 0.5
-LAT_OTHER, LAT_SAME = 0.12, 0.05
-DMA_LAT, DMA_RATE, REM_ISSUE, REM_LAT, REM_RATE, ROW = 2.0, 20e3, 0.8, 2.2, 16e3, 0.03
-U_M, U_POS, U_SIG, U_PHI, U_P1, U_E1, U_E2 = [256 * i for i in range(7)]
-I_1, I_N1, I_H, I_NQ, I_256, I_16, I_4096 = [128 * i for i in range(7)]
-C_PM, C_PM256, C_W, C_WC, C_CS, C_CC, C_CC2 = 0, 1, 2, 12, 16, 20, 24
+CYC, GAM, FIX, PEC = 0.00097, 1.56, 0.055, 0.00049
+LAT_OTHER, LAT_SAME = 0.1, 0.06
+DMA_LAT, DMA_RATE, REM_ISSUE, REM_FIRST, REM_LAT, REM_RATE, ROW = 1.8, 20e3, 0.6, 1.7, 1.9, 16e3, 0.02
+WINDOW, PASSES = 0.2, 2
+WHERE = {"Ga": "VSSV", "Gb": "VVVS", "DS": "S", "Z": "SSVV", "H": "VVSV", "Y": "SVSS",
+         "G1l": "SSVSV", "G1h": "SVSSV", "G1le": "SVSSS", "G1he": "SVSSS", "finl": "VSVVS", "finle": "VSSVS",
+         "HP": "S", "theirs": "VS", "G2l": "SVSS", "G2h": "VSSS", "e1": "V", "lin": "S"}
+
+U_M, U_POS, U_SEL, U_P1, U_E1, U_E2, U_OUT = range(7)
+(I_1, I_256, I_R16, I_16, I_N16, I_N2K, I_4K, I_8K, I_EARLY, I_2K, I_SH, I_WR, I_OFF, I_N1, I_BD) = [128 * i for i in range(15)]
+(C_P, C_PM, C_G16, C_P7, C_Q, C_LAST, C_NLAST, C_P1, C_P15, C_WC, C_WP, C_WE, C_ONE, C_CB, C_CC, C_CS, C_M0, C_M1) = range(18)
+C_BB, C_W0 = 18, 26
+B_KEY, B_P1, B_E1, B_CL = 0, 144, 288, 432
 
 
 def build(g, core, T, topo):
@@ -58,31 +66,31 @@ def build(g, core, T, topo):
 
     def add(name, alts, reads, writes, kind="c", extra=(), info=None):
         k = len(ops)
-        deps = set(extra)
-        eng = list(alts)[0] if len(alts) == 1 else None
+        deps, banks = set(extra), set()
         for lst, wr in ((reads, False), (writes, True)):
-            for (b, lo, hi) in lst:
-                ps = b[0] == "P" and b in SCRATCH and SCRATCH[b][0] == "psum"
-                for (j, l2, h2, w2, e2) in acc.get(b, []):
-                    if j == k:
-                        continue
-                    if (ps and e2 != eng) or ((wr or w2) and l2 < hi and lo < h2):
+            for r in lst:
+                b, lo, hi = r[:3]
+                for (j, l2, h2, w2) in acc.get(b, []):
+                    if j != k and (wr or w2) and l2 < hi and lo < h2:
                         deps.add(j)
-                acc.setdefault(b, []).append((k, lo, hi, wr, eng))
-        ops.append({"name": name, "alts": alts, "deps": deps, "kind": kind, "info": info})
+                acc.setdefault(b, []).append((k, lo, hi, wr))
+                if b in SCRATCH and SCRATCH[b][0] == "psum":
+                    banks.add(b)
+        ops.append({"name": name, "alts": alts, "deps": deps, "kind": kind, "info": info, "banks": sorted(banks),
+                    "pick": None, "after": None, "grp": None})
         return k
 
     def ap(r):
-        if r[0] in ("ab", "land"):
-            if r[2] - r[1] == 2 * PW:
-                return T[r[0]][:, r[1] // (2 * PW), :, :]
-            return T[r[0]][:, r[1] // (2 * PW), r[1] // PW % 2, r[1] % PW:(r[2] - 1) % PW + 1]
-        if r[0] == "abi":
-            return T.abi[:, r[1] // 256, r[1] % 256:(r[2] - 1) % 256 + 1]
+        if r[0] in ("ab", "land") and r[2] - r[1] == 2 * LW:
+            return T[r[0]][:, r[1] // LW:r[2] // LW, :]
+        if r[0] in ("ab", "abi", "land"):
+            return T[r[0]][:, r[1] // LW, r[1] % LW:(r[2] - 1) % LW + 1]
+        if len(r) > 3:
+            return T[r[0]][:, r[1]:r[2]:r[3]]
         return T[r[0]][:, r[1]:r[2]]
 
     def n_(r):
-        return r[2] - r[1]
+        return (r[2] - r[1] + r[3] - 1) // r[3] if len(r) > 3 else r[2] - r[1]
 
     def vcost(n, f=1.0):
         return FIX + max(64, n * f) * CYC
@@ -101,8 +109,17 @@ def build(g, core, T, topo):
             f = lambda: g.vector.tensor_scalar(ap(o), ap(i), sc(s1), sc(s2), op0, op1)
         alts = {"V": (vcost(n_(o), 0.5 if two(o) and two(i) else 1.0), f)}
         if also_s is not None:
-            alts["S"] = (vcost(n_(o)), lambda: g.scalar.activation(ap(o), ap(i), ACT.Identity, bias=also_s[1], scale=also_s[0]))
+            alts["S"] = (vcost(n_(o)), lambda: g.scalar.activation(ap(o), ap(i), ACT.Identity, bias=sc(also_s[1]), scale=sc(also_s[0])))
         return add("ts", alts, rd, [o])
+
+    turn = {}
+
+    def pick(k, name):
+        turn[name] = turn.get(name, -1) + 1
+        ops[k]["pick"] = (name, turn[name])
+
+    def lin(o, i, a, b, name="lin"):
+        pick(ts(o, i, a, b, ALU.mult, ALU.add, also_s=(a, b)), name)
 
     def cp(o, i):
         return add("cp", {"V": (vcost(n_(o), 0.5 if two(o) and two(i) else 1.0), lambda: g.vector.tensor_copy(ap(o), ap(i)))}, [i], [o])
@@ -111,66 +128,57 @@ def build(g, core, T, topo):
         ps = SCRATCH[i0[0]][0] == "psum" or SCRATCH[i1[0]][0] == "psum"
         return add("tt", {"V": (vcost(n_(o), 1.0 if ps else 2.0), lambda: g.vector.tensor_tensor(ap(o), ap(i0), ap(i1), op))}, [i0, i1], [o])
 
-    def act(o, i, func, bias=0.0, scale=1.0, accum=None):
-        rd = [i] + [s for s in (bias, scale) if isinstance(s, tuple)]
+    def act(o, i, func, bias=0.0, accum=None):
+        rd = [i] + ([bias] if isinstance(bias, tuple) else [])
         if accum is None:
-            f = lambda: g.scalar.activation(ap(o), ap(i), func, bias=sc(bias), scale=sc(scale))
-            return add("act", {"S": (vcost(n_(o)), f)}, rd, [o])
-        f = lambda: g.scalar.activation(ap(o), ap(i), func, bias=sc(bias), scale=sc(scale), accum_out=ap(accum))
+            return add("act", {"S": (vcost(n_(o)), lambda: g.scalar.activation(ap(o), ap(i), func, bias=sc(bias), scale=1.0))}, rd, [o])
+        f = lambda: g.scalar.activation(ap(o), ap(i), func, bias=sc(bias), scale=1.0, accum_out=ap(accum))
         return add("act", {"S": (vcost(n_(o)), f)}, rd, [o, accum])
 
-    def ms(o, val):
-        return add("ms", {"V": (vcost(n_(o), 0.5 if two(o) else 1.0), lambda: g.vector.memset(ap(o), val))}, [], [o])
-
-    def gather(o, win, off, engs="VS", bias=0.0, minus=None, rows=None, name="ga"):
+    def gather(o, win, off, name, minus=None, rows=None):
         cost = FIX + n_(o) * GAM * CYC
         src = lambda: ap(win).indirect(ap(off))
-        alts = {}
         rd = [off] + ([win] if rows is None else rows)
         if minus is not None:
-            alts["V"] = (cost, lambda: g.vector.tensor_tensor(ap(o), src(), ap(minus), ALU.subtract))
-            rd.append(minus)
-        else:
-            if "V" in engs:
-                if bias == 0.0:
-                    alts["V"] = (cost, lambda: g.vector.tensor_copy(ap(o), src()))
-                else:
-                    alts["V"] = (cost, lambda: g.vector.tensor_scalar(ap(o), src(), bias, None, ALU.add))
-            if "S" in engs:
-                alts["S"] = (cost, lambda: g.scalar.activation(ap(o), src(), ACT.Identity, bias=bias, scale=1.0))
-        return add(name, alts, rd, [o])
+            return add(name, {"V": (cost, lambda: g.vector.tensor_tensor(ap(o), src(), ap(minus), ALU.subtract))}, rd + [minus], [o])
+        pick(add(name, {"S": (cost, lambda: g.scalar.activation(ap(o), src(), ACT.Identity, bias=0.0, scale=1.0)),
+                        "V": (cost, lambda: g.vector.tensor_copy(ap(o), src()))}, rd, [o]), name)
 
-    def mm(o, terms, f32=False):
+    def mm(o, terms):
         def f():
             ins = None
-            for x, (l, r, c0, st) in enumerate(terms):
-                rhs = T[r[0]][:, r[1] + c0:r[2]:st] if st > 1 else ap(r)
-                ins = g.tensor.matmul(ap(o), ap(l), rhs, x == 0, x == len(terms) - 1)
+            for x, term in enumerate(terms):
+                out = T[o[0]][:, o[1] + term[2]:o[1] + term[3]:term[4]] if len(term) > 2 else ap(o)
+                ins = g.tensor.matmul(out, ap(term[0]), ap(term[1]), x == 0, x == len(terms) - 1)
             return ins
-        cost = FIX + len(terms) * max(64, n_(o)) * PEC * (4 if f32 else 1)
-        rd = list({l for l, r, c0, st in terms}) + list({r for l, r, c0, st in terms})
-        return add("mm", {"P": (cost, f)}, rd, [o])
+        cost = FIX + sum(max(64, n_(x[1])) * PEC * (4 if SCRATCH[x[1][0]][2] == "float32" else 1) for x in terms)
+        return add("mm", {"P": (cost, f)}, list({x[0] for x in terms}) + list({x[1][:3] for x in terms}), [o])
 
-    def wrap(o, b0, src):
-        return mm(o, [(("B", b0 + 15 - i, b0 + 143 - i), src, i, 16) for i in range(16)])
+    def wrap(b0, src):
+        return [(("B", b0 + 15 - i, b0 + 143 - i), (src[0], src[1] + i, src[2], 16)) for i in range(16)]
 
-    def gop(o, i, f, n):
-        return add("g", {"G": (0.17 + 2 * n * CYC, f)}, [i] if i else [], [o])
+    def iota(o, pattern, cm):
+        kw = {} if SCRATCH[o[0]][2] == "int32" else {"allow_small_or_imprecise_dtypes": True}
+        return add("g", {"G": (0.13 + 2 * n_(o) * CYC, lambda: g.iota(ap(o), pattern, 0, cm, **kw))}, [], [o])
 
-    def sel(o, i, pat, cmp, base, cm):
-        return gop(o, i, lambda: g.affine_select(ap(o), ap(i), pat, cmp, 0.0, base, cm), n_(o))
+    groups = {}
 
-    def dma(oap, iap, reads, writes, nbytes, q="Y", rows=128):
-        return add("dma", {q: (0.1, lambda: Q[q].dma_start(oap(), iap()))}, reads, writes, kind="d",
-                   info=DMA_LAT + (nbytes / DMA_RATE + rows * ROW) / 16)
+    def dma(oap, iap, reads, writes, nbytes, grp, q="Y", rows=128):
+        k = add("dma", {q: (0.1, lambda: Q[q].dma_start(oap(), iap()))}, reads, writes, kind="d",
+                info=(nbytes / DMA_RATE + rows * ROW) / 16)
+        ops[k]["grp"] = grp
+        groups.setdefault(grp, []).append((k, writes))
 
-    sent = [0]
-    last = [None]
+    def join(grp):
+        m = groups[grp]
+        add("join", {"X": (0.0, None)}, [], [r for x in m for r in x[1]], kind="a", extra=[x[0] for x in m], info=None)
+
+    sent, last, places_used, bank_turn = [0], [None], [0], [0]
 
     def mask_of(lst):
         return sum(1 << e for e in lst)
 
-    def send(src, dsts, nbytes):
+    def send(src, dsts, nbytes, after=()):
         def f():
             if len(dsts) == 1:
                 c, r, s, e = dsts[0]
@@ -183,101 +191,108 @@ def build(g, core, T, topo):
                                              remote_sem=T.sem[s], src=ap(src), dst=ap(r)))
             return g.remote_dma_fused(trs, local_sem=T.sem.sent)
         sent[0] += sum(len(d[3]) for d in dsts)
-        k = add("send", {"G": (REM_ISSUE, f)}, [src], [], kind="r",
+        k = add("send", {"G": (REM_ISSUE + (REM_FIRST if last[0] is None else 0.0), f)}, [src] + list(after), [], kind="r",
                 info=(nbytes / REM_RATE + 128 * ROW) / min(len(d[3]) for d in dsts))
         ops[k]["after"] = last[0]
+        ops[k]["to"] = (dsts, nbytes)
         last[0] = k
         return k
 
     def arrive(sem, count, sends, rng):
         return add("arr", {"X": (0.0, None)}, [], [rng], kind="a", extra=sends, info=(sem, count))
 
-    partner = [T.cores[rank ^ (1 << t)] for t in range(RO)]
+    def swap(src, other, where, after=()):
+        sem = "fa%d" % places_used[0]
+        places_used[0] += 1
+        k = send(src, [(other, where, sem, topo.engines(core, other))], 256 * n_(src), after)
+        arrive(sem, len(topo.engines(other, core)), [k], where)
 
-    def col(c):
-        return ("col", c, c + 1)
+    partner = [T.cores[rank ^ (1 << t)] for t in range(RO)]
+    high = [rank > (rank ^ (1 << t)) for t in range(RO)]
+
+    def col(c, n=1):
+        return ("col", c, c + n)
 
     def ident(c):
         return ("Id", c, c + 128)
 
-    dma(lambda: T.qi[:, :], lambda: T.ptr[:, :], [], [("qi", 0, 256)], 131072, q="A")
-    for j in range(NG):
-        dma(lambda j=j: T.F0[:, j * GC:(j + 1) * GC], lambda j=j: T.fr[:, j * GC:(j + 1) * GC], [],
-            [("F0", j * GC, (j + 1) * GC)], 256 * GC)
-    wrows = [("Wn%d" % r, 0, W) for r in range(7)]
-    add("ms", {"V": (vcost(W, 0.5), lambda: g.vector.memset(T.Wn[:], 1.0))}, [], wrows)
-    ms(("ones", 0, 512), 1.0)
-    ms(("ones32", 0, 128), 1.0)
-    gop(("coli", 0, 1), None, lambda: g.iota(T.coli[:, 0:1], [[0, 1]], 0, 1), 1)
-    gop(("cf", 0, 256), None, lambda: g.iota(T.cf[:, :], [[1, 256]], 0, 0, allow_small_or_imprecise_dtypes=True), 256)
-    sel(ident(I_1), ("ones", 0, 128), [[-1, 128]], ALU.is_equal, 0, 1)
-    B0 = ("B", 0, 144)
-    sel(B0, ("ones", 0, 144), [[0, 9], [1, 16]], ALU.is_equal, -15, 0)
-    sel(B0, B0, [[1, 144]], ALU.is_ge, 0, -1)
-    sel(B0, B0, [[-1, 144]], ALU.is_ge, 15, 1)
-    SH, WR, SHI, I32 = [("M32", 128 * i, 128 * i + 128) for i in range(4)]
-    sel(SH, ("ones32", 0, 128), [[1, 128]], ALU.is_equal, -1, -1)
-    sel(SH, SH, [[0, 8], [1, 16]], ALU.not_equal, 0, 0)
-    sel(WR, ("ones32", 0, 128), [[1, 128]], ALU.is_equal, 15, -1)
-    sel(WR, WR, [[0, 8], [1, 16]], ALU.is_equal, 0, 0)
-    tt(SHI, SH, ident(I_1), ALU.subtract)
-    for c, s in ((I_N1, -1.0), (I_H, 0.5), (I_NQ, -0.25), (I_256, 256.0), (I_16, 16.0), (I_4096, 4096.0)):
-        ts(ident(c), ident(I_1), s, None, ALU.mult, also_s=(s, 0.0))
-    ts(("coli", 4, 5), ("coli", 0, 1), 15, None, ALU.bitwise_and)
-    cp(col(C_PM), ("coli", 4, 5))
-    ts(col(C_PM256), col(C_PM), 256.0, None, ALU.mult)
-    ts(("posv", 0, 256), ("cf", 0, 256), col(C_PM256), None, ALU.add)
-    cp(("cb", 0, 256), ("cf", 0, 256))
-    for r, w in enumerate((256.0, 1.0, 256.0, 1.0, 1.0, 16.0, 8192.0)):
-        ts(col(C_W + r), col(C_PM), float(r), w, ALU.is_equal, ALU.mult)
-    tt(col(C_WC), col(C_W), col(C_W + 1), ALU.add)
-    tt(col(C_WC + 1), col(C_W + 2), col(C_W + 3), ALU.add)
-    tt(col(C_WC + 3), col(C_W + 4), col(C_W + 5), ALU.add)
-    tt(col(C_WC + 2), col(C_WC + 3), col(C_W + 6), ALU.add)
-    for x in range(3):
-        act(("B", 144 * (x + 1), 144 * (x + 2)), B0, ACT.Identity, scale=col(C_WC + x))
-    B_CL, B_G1, B_G2 = 144, 288, 432
+    def u16(x, c0=0, c1=LW):
+        return ("u16", x * LW + c0, x * LW + c1)
 
-    def send_frame(t, x0, x1):
-        e = topo.engines(core, partner[t])
-        return send(("F%d" % t, x0, x1), [(partner[t], ("XP%d" % t, x0, x1), "fa%d" % t, e)], 256 * (x1 - x0))
+    def lb(x, c0=0, c1=LW):
+        return ("lb", x * LW + c0, x * LW + c1)
 
-    def frame_arrives(t, sends):
-        arrive("fa%d" % t, len(sends) * len(topo.engines(partner[t], core)), sends, ("XP%d" % t, 0, W))
+    def lf(x, c0=0, c1=LW):
+        return ("lf", x * LW + c0, x * LW + c1)
+
+    def dig(s, x, c0=0, c1=LW):
+        return ("ab", 512 * s + LW * x + c0, 512 * s + LW * x + c1)
+
+    def px():
+        bank_turn[0] += 1
+        return "Px%d" % (bank_turn[0] % 3)
+
+    wrows = [("Wn%d" % r, 0, W) for r in range(6)]
+
+    dma(lambda: T.qi[:, :], lambda: T.ptr[:, :], [], [("qi", 0, LW)], 131072, "ptr", q="A")
+    for j in range(len(LOAD) - 1):
+        x0, x1 = LOAD[j], LOAD[j + 1]
+        dma(lambda x0=x0, x1=x1: T.F0[:, x0:x1], lambda x0=x0, x1=x1: T.fr[:, x0:x1], [], [("F0", x0, x1)], 256 * (x1 - x0), "fr%d" % j)
+    for j in range(2):
+        add("ms", {"V": (vcost(W // 2, 0.5), lambda j=j: g.vector.memset(T.Wn[:, j * W // 2:(j + 1) * W // 2], 1.0))}, [],
+            [(r[0], j * W // 2, (j + 1) * W // 2) for r in wrows])
+    iota(("coli", 0, 1), [[0, 1]], 1)
+    iota(("row", 0, LW), [[1, LW]], 0)
+    for x, m in ((C_P, 127), (C_PM, 15), (C_G16, 112), (C_P7, 7)):
+        ts(("coli", 4 + x, 5 + x), ("coli", 0, 1), m, None, ALU.bitwise_and)
+    cp(col(C_P, 4), ("coli", 4 + C_P, 8 + C_P))
+    R128 = ("row", 0, 128)
+    ts(ident(I_1), R128, col(C_P), None, ALU.is_equal)
+    for c, s in ((I_256, 256.0), (I_R16, 0.0625)):
+        lin(ident(c), ident(I_1), s, 0.0)
+    lin(("ones", 0, LW), ("row", 0, LW), 0.0, 1.0)
+    lin(col(C_Q), col(C_G16), 1.0, 15.0)
+    for c, l, wa, wb in ((C_WE, 2, 1.0, 1.0), (C_WP, 1, 256.0, 0.0625), (C_WC, 0, 1.0, 1.0)):
+        ts(col(C_W0 + l), col(C_PM), 2.0 * l, wa / 8192, ALU.is_equal, ALU.mult)
+        ts(col(c), col(C_PM), 2.0 * l + 1, wb / 8192, ALU.is_equal, ALU.mult)
+        lin(col(c), col(c), 1.0, col(C_W0 + l))
+    ts(("B", B_KEY, B_KEY + 144), ("row", 0, 144), col(C_Q), 8192.0, ALU.is_equal, ALU.mult)
+    for b, c in ((B_E1, C_WE), (B_P1, C_WP), (B_CL, C_WC)):
+        lin(("B", b, b + 144), ("B", B_KEY, B_KEY + 144), col(c), 0.0)
+    ts(col(C_LAST), col(C_PM), 15.0, None, ALU.is_equal)
+    lin(col(C_NLAST), col(C_LAST), -1.0, 1.0)
+    lin(col(C_P1), col(C_P), 1.0, 1.0)
+    lin(col(C_P15), col(C_P), 1.0, -15.0)
+    for c, a, b in ((I_SH, C_P1, C_NLAST), (I_WR, C_P15, C_LAST)):
+        ts(ident(c), R128, col(a), col(b), ALU.is_equal, ALU.mult)
+
+    def set_count(c):
+        lin(col(C_CB), c, 1.0, -4095.5)
+        lin(("cc", 0, LW), ("ones", 0, LW), c, 0.0)
+
+    lin(col(C_ONE), col(C_P), 0.0, 1.0)
+    set_count(col(C_ONE))
+    for c, s in ((I_N2K, -2048.0), (I_OFF, -OFF), (I_N1, -1.0), (I_4K, 4096.0), (I_2K, 2048.0)):
+        lin(ident(c), ident(I_1), s, 0.0)
+    lin(("I32", 0, 128), ident(I_1), 1.0, 0.0)
+    for c, s in ((I_16, 16.0), (I_N16, -16.0)) + (((I_8K, 8192.0),) if any(high) else ()):
+        lin(ident(c), ident(I_1), s, 0.0)
+    if not all(high):
+        lin(ident(I_EARLY), ident(I_1), float(EARLY), 0.0)
+        ts(("Hf", 0, 128), ident(I_1), 0.5 - 1.0 / 2048, None, ALU.mult)
+    lin(("cb", 0, LW), ("row", 0, LW), 1.0, 0.0)
+    lin(("ones32", 0, 128), R128, 0.0, 1.0)
+    if any(high):
+        iota(("blk", 0, 128), [[16, 8], [0, 16]], 0)
+        ts(ident(I_BD), ("blk", 0, 128), col(C_G16), None, ALU.is_equal)
+        ts(col(C_BB, 8), ("row", 0, 8), col(C_P7), 256.0, ALU.is_equal, ALU.mult)
+        for i in range(8):
+            lin(("BB", 128 * i, 128 * i + 128), ident(I_BD), col(C_BB + i), 0.0)
+        ts(col(C_M0), col(C_PM), 8.0, None, ALU.is_ge)
+        lin(col(C_M1), col(C_M0), -1.0, 1.0)
+
+    def pad(t):
         act(("XP%d" % t, W, W + 16), ("XP%d" % t, 0, 16), ACT.Identity)
-
-    def digits(s, c0, c1, high, bank):
-        a0 = 512 * s + PW * (c0 // PW)
-        w = c1 - c0
-        ai, bi = ("abi", c0, c1), ("abi", 256 + c0, 256 + c1)
-        ts(ai, ("qi", c0, c1), 15, None, ALU.bitwise_and)
-        ts(bi, ("qi", c0, c1), 4, 255, ALU.arith_shift_right, ALU.bitwise_and)
-        a, b = ("ab", a0 + c0, a0 + c1), ("ab", a0 + PW + c0, a0 + PW + c1)
-        add("cp", {"V": (vcost(2 * w), lambda: g.vector.tensor_copy(
-            T.ab[:, NP * s + c0 // PW, :, c0 % PW:c0 % PW + w], T.abi[:, :, c0:c1]))}, [ai, bi], [a, b])
-        if high:
-            ts(("ki", c0, c1), ("qi", c0, c1), 13, None, ALU.arith_shift_right)
-            cp(("kb", c0, c1), ("ki", c0, c1))
-            pb = (bank, c0, c1)
-            mm(pb, [(ident(I_4096), ("kb", c0, c1), 0, 1), (ident(I_16), ("cb", c0, c1), 0, 1)])
-            ts(("u16", U_SIG + c0, U_SIG + c1), pb, col(C_PM), None, ALU.add)
-        mm(("Pm", 2 * c0, 2 * c0 + w), [(ident(I_1), a, 0, 1), (ident(I_16), b, 0, 1)])
-        mm(("Pm", 2 * c0 + w, 2 * c1), [(ident(I_256), a, 0, 1), (ident(I_1), b, 0, 1)])
-        cp(("u16", U_M + 2 * c0, U_M + 2 * c1), ("Pm", 2 * c0, 2 * c1))
-        act(("e0x", 8 + c0, 8 + c1), ("Pm", 2 * c0, 2 * c0 + w), ACT.Identity)
-        if c1 == 256 and s < RO:
-            act(("e0x", 7, 8), ("Pm", 2 * c0 + w - 1, 2 * c0 + w), ACT.Identity)
-
-    def u_m(o0, o1, pos=0):
-        c0, c1 = [c for c in CHOICE if c[0] <= o0 < c[1]][0]
-        x = U_M + c0 + pos * (c1 - c0)
-        return ("u16", x + o0, x + o1)
-
-    def rows(buf, sl, p, r):
-        for x in range(2):
-            if p == NP - 1:
-                dma(lambda x=x: T.Wn[r + x::16, :], lambda x=x: T[buf][:, NP * sl:NP * sl + NP, x, :],
-                    [(buf, 512 * sl, 512 * sl + 512)], [wrows[r + x]], 65536, rows=128 * NP)
 
     def engines_for(src, s):
         r = T.rank_of(src)
@@ -291,228 +306,293 @@ def build(g, core, T, topo):
         h = len(es[0]) // 2
         return [es[0][:h], es[1][h:]]
 
-    def exchange(s, p):
-        ts_ = [t for t in (s - 1, s) if 0 <= t < RO]
-        slot = {t: 2 * s - 1 + (t - (s - 1)) for t in ts_}
+    def rows(buf, x0, l, grp):
+        for x in range(2):
+            src = (buf, x0 + LW * x, x0 + LW * x + LW)
+            dma(lambda x=x: T.Wn[2 * l + x::16, :], lambda src=src: ap(src), [src], [wrows[2 * l + x]], 65536, grp)
+
+    def digits(s, c0, c1):
+        ai, bi = ("abi", c0, c1), ("abi", LW + c0, LW + c1)
+        ts(ai, ("qi", c0, c1), 15, None, ALU.bitwise_and)
+        ts(bi, ("qi", c0, c1), 4080, None, ALU.bitwise_and)
+        add("cp", {"V": (vcost(2 * (c1 - c0)), lambda: g.vector.tensor_copy(T.ab[:, 2 * s:2 * s + 2, c0:c1], T.abi[:, :, c0:c1]))},
+            [ai, bi], [dig(s, 0, c0, c1), dig(s, 1, c0, c1)])
+
+    def offsets(s):
+        frame = s < RO or not high[s - 1]
+        bank = "PQ" if s and frame else "PM"
+        if not s:
+            mm((bank, LW, 512), [(ident(I_256), dig(s, 0)), (ident(I_R16), dig(s, 1))])
+            cp(u16(U_OUT), (bank, LW, 512))
+        if s and not frame:
+            mm((bank, LW, 512), [(ident(I_256), dig(s, 0)), (ident(I_R16), dig(s, 1))])
+            cp(u16(U_POS), (bank, LW, 512))
+        mm(("PM", 0, LW), [(ident(I_1), dig(s, 0)), (ident(I_1), dig(s, 1))])
+        if frame:
+            cp(u16(U_M), ("PM", 0, LW))
+        if s and frame:
+            mm((bank, LW, 512), [(ident(I_256), dig(s, 0)), (ident(I_R16), dig(s, 1))])
+            cp(u16(U_POS), (bank, LW, 512))
+        if s == RO:
+            act(lf(2), ("PM", 0, LW), ACT.Identity)
+            dma(lambda: T.yp[:, :], lambda: ap(lf(2)), [lf(2)], [], 131072, "out")
+
+    def exchange(s):
+        ts_ = [t for t in (s - 1, s) if t < RO]
+        sl = {t: 2 * s - 2 + (t - (s - 1)) for t in ts_}
+        where = {t: ("land", 512 * sl[t], 512 * sl[t] + 512) for t in ts_}
         es = engines_for(core, s)
-        where = {t: ("land", 512 * slot[t] + 2 * PW * p, 512 * slot[t] + 2 * PW * (p + 1)) for t in ts_}
-        k = send(("ab", 512 * s + 2 * PW * p, 512 * s + 2 * PW * (p + 1)),
-                 [(partner[t], where[t], "lp%d" % (2 * slot[t] + p), es[x]) for x, t in enumerate(ts_)], 512 * PW)
-        for x, t in enumerate(ts_):
-            arrive("lp%d" % (2 * slot[t] + p), len(engines_for(partner[t], s)[x]), [k], where[t])
+        k = send(("ab", 512 * s, 512 * s + 512), [(partner[t], where[t], "lp%d" % sl[t], es[x]) for x, t in enumerate(ts_)], 131072)
+        offsets(s)
         if s < RO:
-            rows("ab", s, p, 4)
+            rows("ab", 512 * s, 2, "rows%d" % s)
         for x, t in enumerate(ts_):
-            rows("land", slot[t], p, 0 if t == s - 1 else 2)
+            arrive("lp%d" % sl[t], len(engines_for(partner[t], s)[x]), [k], where[t])
+            rows("land", 512 * sl[t], x, "rows%d" % s)
+        join("rows%d" % s)
 
-    def chain(j):
-        c0, c1 = j * GC // 16, (j + 1) * GC // 16
-        pb = ("Pw%d" % (j & 1), 256 + c0, 256 + c1)
-        wrap(pb, B_G1, ("G1", j * GC, (j + 1) * GC))
-        cp(("u16", U_P1 + c0, U_P1 + c1), pb)
+    def second(x0, x1, end):
+        mm(("PE", x0 // 16, x1 // 16), wrap(B_E1, ("G2", x0, x1)))
+        cp(u16(U_E1, x0 // 16, x1 // 16), ("PE", x0 // 16, x1 // 16))
+        if end:
+            lin(lf(0), ("PE", 0, LW), 1.0, 4096.0 - OFF, "e1")
 
-    def chain2(j):
-        c0, c1 = j * GC // 16, (j + 1) * GC // 16
-        gather(("G2", j * GC, (j + 1) * GC), ("Wn", 0, W), ("u16", U_P1 + c0, U_P1 + c1), rows=wrows, name="G2")
-        wrap(("Pq", c0, c1), B_G2, ("G2", j * GC, (j + 1) * GC))
-        ts(("u16", U_E1 + c0, U_E1 + c1), ("Pq", c0, c1), -8192.0, None, ALU.add)
+    def before(t, c0, c1):
+        terms = []
+        for x in (1, 0):
+            terms.append((ident(I_SH), dig(t, x, c0, c1)))
+            if c0:
+                terms.append((ident(I_WR), dig(t, x, c0 - 1, c1 - 1)))
+            else:
+                terms.append((ident(I_WR), dig(t, x, 0, c1 - 1), 1, c1, 1))
+                terms.append((ident(I_WR), dig(t, x, LW - 1, LW), 0, 1, 1))
+        return terms
 
-    def last_candidate(t):
-        for pb, m0 in ((("Px0", 0, 256), SH), (("Px1", 0, 256), SHI)):
-            mm(pb, [(m0, ("e0x", 8, 264), 0, 1), (WR, ("e0x", 7, 263), 0, 1)], f32=True)
-        ts(("u16", U_E2, U_E2 + 256), ("Px0", 0, 256), col(C_CC) if t else 1.0, None, ALU.add)
-        act(("dl2", 0, 256), ("Px1", 0, 256), ACT.Identity, bias=col(C_CC2) if t else 16385.0)
+    def third(t):
+        if t:
+            set_count(col(C_CC))
+        pe = ("PE", LW, 512)
+        mm(pe, before(t, 0, LW))
+        ts(u16(U_E2), pe, col(C_CC if t else C_ONE), None, ALU.add)
+        act(lb(0), pe, ACT.Sign, bias=col(C_CB))
 
-    def ptr_gather(x0, x1):
-        gather(("G1", x0, x1), ("Wn", 0, W), u_m(x0 // 16, x1 // 16, 1), rows=wrows, name="G1")
+    digits(0, 0, LW)
+    offsets(0)
+    rows("ab", 0, 2, "rows0")
+    join("rows0")
+    for j in range(len(LOAD) - 1):
+        swap(("F0", LOAD[j], LOAD[j + 1]), partner[0], ("XP0", LOAD[j], LOAD[j + 1]))
+        if j == 0:
+            pad(0)
+            k = send(u16(U_OUT), [(partner[0], ("lu", 0, LW), "lp5", engines_for(core, 0)[0])], 65536)
+            arrive("lp5", len(engines_for(partner[0], 0)[0]), [k], ("lu", 0, LW))
+    for x0 in range(0, W, GC):
+        gather(("G1", x0, x0 + GC), ("Wn", 0, W), ("lu", x0 // 16, (x0 + GC) // 16), "Ga", rows=wrows)
+    for x0 in range(0, W, GC):
+        gather(("G2", x0, x0 + GC), ("G1", 0, W), u16(U_M, x0 // 16, (x0 + GC) // 16), "Gb")
+        second(x0, x0 + GC, x0 + GC == W)
 
-    for c0, c1 in CHOICE:
-        digits(0, c0, c1, False, None)
-        if c1 % PW == 0:
-            exchange(0, c1 // PW - 1)
-    frame_arrives(0, [send_frame(0, j * GC, (j + 1) * GC) for j in range(NG)])
-    last_candidate(0)
-    for j in range(NG):
-        ptr_gather(j * GC, (j + 1) * GC)
-        chain(j)
-    for j in range(NG):
-        chain2(j)
-
-    slot = [0, 0]
     for t in range(RO):
-        high = rank > (rank ^ (1 << t))
-        F, XP, FN = "F%d" % t, "XP%d" % t, "F%d" % (t + 1)
-        win = (XP, 0, W + 16)
-        done = 0
-        for ci, (c0, c1) in enumerate(CHOICE):
-            pd, pw = "Pd%d" % (ci & 1), "Pw%d" % (ci & 1)
-            w = c1 - c0
-            for j in range(c0 * 16 // GC, c1 * 16 // GC):
-                x0, x1, o0 = j * GC, (j + 1) * GC, j * GC // 16
-                for k, u in ((2, U_E2), (0, U_M), (1, U_E1)):
-                    off = ("u16", u + o0, u + o0 + GC // 16) if k else u_m(o0, o0 + GC // 16)
-                    if (k, j) in XPATH:
-                        gather(("Y", x0, x1), win, off, engs="S", name="Yx")
-                        for p in range(x0, x1, 512):
-                            px = ("Px%d" % (slot[0] & 1), 0, 512)
-                            slot[0] += 1
-                            mm(px, [(ident(I_1), ("Y", p, p + 512), 0, 1), (ident(I_N1), (F, p, p + 512), 0, 1)])
-                            act(("A", k * W + p, k * W + p + 512), px, ACT.Abs)
-                    else:
-                        d = ("D", (slot[1] % NG) * GC, (slot[1] % NG + 1) * GC)
-                        slot[1] += 1
-                        gather(d, win, off, minus=(F, x0, x1), name="D")
-                        act(("A", k * W + x0, k * W + x1), d, ACT.Abs)
-                    y0 = (0, 256, 256)[k] + o0 - c0
-                    wrap((pw if k == 1 else pd, y0, y0 + GC // 16), 0, ("A", k * W + x0, k * W + x1))
-            d0, d1, d2, ps = (pd, 0, w), (pw, 256, 256 + w), (pd, 256, 256 + w), (pw, 384, 384 + w)
-            t0, t1, t2, t3 = [("tmp", 256 * k + c0, 256 * k + c1) for k in range(4)]
-            ts(t0, d0, -1.0, None, ALU.add)
-            tt(d0, d2, t0, ALU.is_le)
-            tt(t1, d2, t0, ALU.min)
-            tt(d2, d0, ("dl2", c0, c1), ALU.mult)
-            tt(t2, d2, ("e0x", 8 + c0, 8 + c1), ALU.add)
-            tt(t3, ("Pq", c0, c1), t2, ALU.subtract)
-            tt(ps, d1, t1, ALU.is_le)
-            tt(d1, ps, t3, ALU.mult)
-            tt(("qi", c0, c1), d1, t2, ALU.add)
-            digits(t + 1, c0, c1, high, pw)
-            if c1 % PW == 0:
-                exchange(t + 1, c1 // PW - 1)
-        if t == RO - 1:
-            dma(lambda: T.yp[:, :], lambda: T.e0x[:, 8:264], [("e0x", 8, 264)], [], 131072)
-        for j in range(NG):
-            x0, x1, o0 = j * GC, (j + 1) * GC, j * GC // 16
-            if high:
-                z = ("HZ", W + x0, W + x1)
-                gather(z, ("A", 0, 3 * W), ("u16", U_SIG + o0, U_SIG + o0 + GC // 16), bias=-256.0, name="Z")
-                ts(("HZ", x0, x1), z, 0.5, -128.25, ALU.mult, ALU.add, also_s=(0.5, -128.25))
+        F, XP, FN, XN, Y = "F%d" % t, "XP%d" % t, "F%d" % (t + 1), "XP%d" % (t + 1), "Y%d" % t
+        win, ep = (XP, 0, W + 16), ("EP", 2 * EARLY * t, 2 * EARLY * (t + 1))
+        more_rounds = t + 1 < RO
+        role = "lh"[high[t]] + ("" if more_rounds else "e")
+        if more_rounds and not high[t]:
+            swap((F, 0, EARLY), partner[t + 1], (ep[0], ep[1], ep[1] + EARLY))
+        third(t)
+        keys = [("PKa", 0, LW), ("PKa", LW, 512), ("PKb", 0, LW), ("PKb", LW, 512)]
+        for k in range(3):
+            for j in range(len(CAND[k]) - 1):
+                x0, x1 = CAND[k][j], CAND[k][j + 1]
+                c0, c1 = x0 // 16, x1 // 16
+                a, off = ("A", k * W + x0, k * W + x1), u16((U_M, U_E1, U_E2)[k], c0, c1)
+                if (k, j) in XPATH[t]:
+                    gather(a, win, off, "DS")
+                    for p in range(x0, x1, 512):
+                        pb, piece = (px(), 0, 512), ("A", k * W + p, k * W + p + 512)
+                        mm(pb, [(ident(I_1), piece), (ident(I_N1), (F, p, p + 512))])
+                        act(piece, pb, ACT.Abs)
+                else:
+                    gather(a, win, off, "D", minus=(F, x0, x1))
+                    act(a, a, ACT.Abs)
+                one = ("ones", 0, c1 - c0)
+                more = [[(ident(I_OFF), one), (ident(I_1), dig(t, 1, c0, c1)), (ident(I_1), dig(t, 0, c0, c1))],
+                        [(("I32", 0, 128), lf(0, c0, c1))],
+                        [(ident(I_OFF), one), (ident(I_N2K), lb(0, c0, c1)), (ident(I_2K), one),
+                         (ident(I_1), ("cc", c0, c1))] + before(t, c0, c1)][k]
+                mm((keys[k][0], keys[k][1] + c0, keys[k][1] + c1), wrap(B_KEY, a) + more)
+        k0, k1, k2, beats = keys
+        copy0, least, cleared = lf(1), ("wi", 0, LW), ("wi", LW, 2 * LW)
+        act(copy0, k0, ACT.Identity)
+        tt(least, k1, copy0, ALU.min)
+        ts(cleared, least, -4097, None, ALU.bitwise_and)
+        if high[t]:
+            tt(beats, k1, copy0, ALU.is_lt)
+        for c0, c1 in CHOICE:
+            tt(("qi", c0, c1), ("PKb", c0, c1), ("wi", LW + c0, LW + c1), ALU.min)
+            digits(t + 1, c0, c1)
+        exchange(t + 1)
+        if high[t]:
+            tt(lb(1), k2, cleared, ALU.is_lt)
+            tt(lb(2), beats, lb(1), ALU.is_gt)
+            mm(k0, [(ident(I_16), ("cb", 0, LW)), (ident(I_8K), lb(1)), (ident(I_4K), lb(2))])
+            ts(u16(U_SEL), k0, col(C_PM), None, ALU.add)
+        for x0 in range(0, W, GC):
+            x1 = x0 + GC
+            if high[t]:
+                gather((Y, x0, x1), ("A", 0, 3 * W), u16(U_SEL, x0 // 16, x1 // 16), "Z")
+                lin(("H", x0, x1), (Y, x0, x1), 0.5, -256.25, "H")
             else:
-                gather(("Y", x0, x1), win, u_m(o0, o0 + GC // 16), name="Y")
+                gather((Y, x0, x1), win, u16(U_M, x0 // 16, x1 // 16), "Y")
                 for p in range(x0, x1, 512):
-                    px = ("Px%d" % (slot[0] & 1), 0, 512)
-                    slot[0] += 1
-                    mm(px, [(ident(I_H), ("Y", p, p + 512), 0, 1), (ident(I_H), (F, p, p + 512), 0, 1),
-                            (ident(I_NQ), ("ones", 0, 512), 0, 1)])
-                    ts((F, W + p, W + p + 512), px, MAGIC, -MAGIC, ALU.add, ALU.add)
-        sends = []
-        for j in range(len(LIFT[t]) - 1):
-            x0, x1 = LIFT[t][j], LIFT[t][j + 1]
+                    pb = (px(), 0, 512)
+                    mm(pb, [(("Hf", 0, 128), (Y, p, p + 512)), (("Hf", 0, 128), (F, p, p + 512))])
+                    ts((F, W + p, W + p + 512), pb, MAGIC, -MAGIC, ALU.add, ALU.add)
+        if more_rounds:
+            swap((Y, 0, EARLY) if high[t] else (F, W, W + EARLY), partner[t + 1], (ep[0], ep[1] + EARLY, ep[2]), after=wrows)
+
+        for j, (x0, x1) in enumerate(LIFT[t]):
             c0, c1 = x0 // 16, x1 // 16
-            ptr_gather(x0, x1)
-            pb = ("Pw%d" % (j & 1), c0, c1)
-            wrap(pb, B_CL, ("G1", x0, x1))
-            tt(("con", c0, c1), pb, ("posv", c0, c1), ALU.is_equal)
-            pf = ("Pd%d" % (j & 1), c0, c1)
-            mm(pf, [(ident(I_4096), ("con", c0, c1), 0, 1), (ident(I_16), ("cb", c0, c1), 0, 1)])
-            phi = ("u16", U_PHI + c0, U_PHI + c1)
-            ts(phi, pf, col(C_PM), None, ALU.add)
-            if high:
-                gather((FN, x0, x1), ("HZ", 0, 2 * W), phi, bias=256.0, name="fin")
+            gather(("G1", x0, x1), ("Wn", 0, W), u16(U_POS, c0, c1), "G1" + role, rows=wrows)
+            back = ("PQ" if j & 1 else "PM", c0, c1)
+            mm(back, wrap(B_CL, ("G1", x0, x1)) + [(ident(I_N16), ("cb", c0, c1))])
+            if high[t]:
+                for b in range(2):
+                    ts(("con", 512 * t + 2 * c0 + b, 512 * t + 2 * c1, 2), back, col(C_PM), col(C_M0 + b), ALU.is_equal, ALU.max)
             else:
-                gather((FN, x0, x1), (F, 0, 2 * W), phi, name="fin")
-            if t + 1 < RO:
-                sends.append(send_frame(t + 1, x0, x1))
+                ts(("con", 512 * t + c0, 512 * t + c1), back, col(C_PM), None, ALU.is_equal)
+
+        def smaller(out, z, h, flags, x0, x1):
+            for p in range(x0, x1, 512):
+                pb, n64 = (px(), 0, 512), (flags[0], flags[1] + p // 8, flags[1] + p // 8 + 64)
+                mm(pb, [(ident(I_1), (h, p, p + 512))] + [(("BB", 128 * i, 128 * i + 128), n64, i, 512, 8) for i in range(8)])
+                tt((out, p, p + 512), pb, (z[0], z[1] + p, z[1] + p + 512), ALU.min)
+
+        def places(out, bank, x0, x1, second_half):
+            pf = (bank, x0 // 16, x1 // 16)
+            mm(pf, [(second_half, ("con", 512 * t + x0 // 16, 512 * t + x1 // 16)), (ident(I_16), ("cb", x0 // 16, x1 // 16))])
+            ts(out, pf, col(C_PM), None, ALU.add)
+
+        mine, theirs = u16(U_OUT + 1 + t, 0, EARLY // 16), LW + LW * t
+        for j, (x0, x1) in enumerate(LIFT[t]):
+            if high[t]:
+                smaller(FN, (Y, 0), "H", ("con", 512 * t), x0, x1)
             else:
-                dma(lambda x0=x0, x1=x1: T.yf[:, x0:x1], lambda x0=x0, x1=x1: T.F3[:, x0:x1], [(FN, x0, x1)], [], 256 * (x1 - x0))
-        if t + 1 < RO:
-            for j in range(NG):
-                chain(j)
-            act(("junk", 0, 256), ("con", 0, 256), ACT.Identity, accum=col(C_CS))
-            mm(("Px0", 0, 1), [(("ones32", 0, 128), col(C_CS), 0, 1)], f32=True)
-            cp(("coli", 8, 9), ("Px0", 0, 1))
+                places(u16(U_SEL, x0 // 16, x1 // 16), "PKa", x0, x1, ident(I_4K))
+                gather((FN, x0, x1), (F, 0, 2 * W), u16(U_SEL, x0 // 16, x1 // 16), "fin" + role)
+            if not more_rounds:
+                dma(lambda x0=x0, x1=x1: T.yf[:, x0:x1], lambda x0=x0, x1=x1: T.F3[:, x0:x1], [(FN, x0, x1)], [], 256 * (x1 - x0), "out")
+                continue
+            if x0 >= EARLY:
+                swap((FN, x0, x1), partner[t + 1], (XN, x0, x1))
+            if j == TELL and high[t]:
+                swap(("con", 512 * t, 512 * t + EARLY // 8), partner[t + 1], ("lc", 256 * t, 256 * t + EARLY // 8))
+            elif j == TELL:
+                places(mine, "PKb", 0, EARLY, ident(I_EARLY))
+                swap(mine, partner[t + 1], ("lu", theirs, theirs + EARLY // 16))
+            if x1 == W:
+                if high[t]:
+                    lin(("HP", 0, EARLY), (ep[0], ep[1] + EARLY, ep[2]), 0.5, -256.25, "HP")
+                    smaller(XN, (ep[0], ep[1] + EARLY), "HP", ("lc", 256 * t), 0, EARLY)
+                else:
+                    for x in (0, EARLY // 2):
+                        gather((XN, x, x + EARLY // 2), ep, ("lu", theirs + x // 16, theirs + (x + EARLY // 2) // 16), "theirs")
+                pad(t + 1)
+        if more_rounds:
+            n = 2 * LW if high[t] else LW
+            act(("lb", 3 * LW, 3 * LW + n), ("con", 512 * t, 512 * t + n), ACT.Identity, accum=col(C_CS))
+            mm(("PQ", LW, LW + 1), [(("ones32", 0, 128), col(C_CS))])
+            cp(("coli", 8, 9), ("PQ", LW, LW + 1))
             ts(("coli", 12, 13), ("coli", 8, 9), 3, None, ALU.bitwise_and)
             ts(col(C_CC), ("coli", 12, 13), 1.0, None, ALU.add)
-            ts(col(C_CC2), ("coli", 12, 13), 16385.0, None, ALU.add)
-            last_candidate(t + 1)
-            for j in range(NG):
-                chain2(j)
-            frame_arrives(t + 1, sends)
+            for j, x0 in enumerate(list(range(EARLY, W, GC)) + list(range(0, EARLY, GC))):
+                x1, c0, c1 = x0 + GC, x0 // 16, (x0 + GC) // 16
+                mm(("PKb", c0, c1), wrap(B_P1, ("G1", x0, x1)))
+                cp(u16(U_P1, c0, c1), ("PKb", c0, c1))
+                gather(("G2", x0, x1), ("Wn", 0, W), u16(U_P1, c0, c1), "G2" + role, rows=wrows)
+                second(x0, x1, j == W // GC - 1)
     return ops, Q, sent[0]
 
 
 def schedule(ops):
     n = len(ops)
-    succ = [[] for _ in range(n)]
-    nxt = {}
+    eng = [WHERE[o["pick"][0]][o["pick"][1] % len(WHERE[o["pick"][0]])] if o["pick"] else list(o["alts"])[0] for o in ops]
+    queue = ["S" if e == "A" else e for e in eng]
+    succ, pred, above = [[] for _ in range(n)], [[] for _ in range(n)], []
     for k, o in enumerate(ops):
+        implied = set()
         for d in o["deps"]:
-            succ[d].append(k)
-        if o.get("after") is not None:
-            nxt[o["after"]] = k
-    base = [0.0] * n
-    for k in range(n - 1, -1, -1):
-        o = ops[k]
-        own = min(c for c, f in o["alts"].values())
-        if o["kind"] == "d":
-            own += o["info"]
-        if o["kind"] == "r":
-            own += REM_LAT + o["info"]
-        base[k] = own + LAT_OTHER + max([base[s] for s in succ[k]] + [0.0])
-        if k in nxt:
-            base[k] = max(base[k], o["info"] + base[nxt[k]])
-    alts = [[(e, "S" if e == "A" else e, c) for e, (c, f) in o["alts"].items()] for o in ops]
-    either = [k for k in range(n) if len(alts[k]) > 1]
+            implied |= above[d]
+        above.append(implied | o["deps"])
+        for d in sorted((o["deps"] - implied) | ({o["after"]} - {None})):
+            succ[d].append((k, d in o["deps"]))
+            pred[k].append((d, d in o["deps"]))
 
-    def plan(prio, bias):
-        free = {"V": 0.0, "S": 0.0, "P": 0.0, "G": 0.0, "Y": 0.0, "X": 0.0, "link": 0.0, "dma": 0.0}
-        left = [len(o["deps"]) for o in ops]
-        end, eng, start = [0.0] * n, [None] * n, [0.0] * n
-        rdy = [[0.0] * len(a) for a in alts]
-        ready = [k for k in range(n) if left[k] == 0]
-        order = []
-        while ready:
-            cands = []
-            t0 = 1e9
-            for k in ready:
-                best = None
-                for x, (e, qn, c) in enumerate(alts[k]):
-                    s = max(free[qn], rdy[k][x])
-                    fin = s + c + (bias[k] if e == "V" else 0.0)
-                    if best is None or fin < best[3]:
-                        best = (s, e, c, fin, qn, k)
-                cands.append(best)
-                if best[0] < t0:
-                    t0 = best[0]
-            s, e, c, fin, qn, k = max((x for x in cands if x[0] <= t0 + WINDOW), key=lambda x: (prio[x[5]], -x[5]))
-            o = ops[k]
-            start[k], eng[k] = s, e
-            if e != "X":
-                free[qn] = s + c
-            end[k] = s + c
-            if o["kind"] == "d":
-                free["dma"] = max(free["dma"], s + c + DMA_LAT) + o["info"] - DMA_LAT
-                end[k] = free["dma"]
-            if o["kind"] == "r":
-                free["link"] = max(free["link"], s + c + REM_LAT) + o["info"]
-                end[k] = free["link"]
+    def forward(urge):
+        left, rdy, start, end = [len(p) for p in pred], [0.0] * n, [0.0] * n, [0.0] * n
+        free = {q: 0.0 for q in "VSPGYXM"}
+        ready = {q: [k for k in range(n) if queue[k] == q and left[k] == 0] for q in "VSPGYX"}
+        bank, order = {}, []
+        for _ in range(n):
+            t0, q = min((max(free[q], min([rdy[k] for k in l])), q) for q, l in ready.items() if l)
+            k = min((urge[k], k) for k in ready[q] if rdy[k] <= t0 + WINDOW)[1]
+            o, e, t = ops[k], eng[k], max(rdy[k], t0)
+            for b in o["banks"]:
+                if b in bank and bank[b][1] != e:
+                    t = max(t, bank[b][0])
+            start[k], issued = t, t + o["alts"][e][0]
+            end[k] = issued
+            if q != "X":
+                free[q] = issued
+            for b in o["banks"]:
+                bank[b] = (issued + LAT_OTHER, e)
+            if o["kind"] in "dr":
+                free["M"] = end[k] = max(free["M"], issued + (DMA_LAT if o["kind"] == "d" else REM_LAT)) + o["info"]
+            ready[q].remove(k)
             order.append(k)
-            ready.remove(k)
-            for x in succ[k]:
-                for y, a in enumerate(alts[x]):
-                    v = end[k] + (LAT_SAME if a[0] == e else LAT_OTHER)
-                    if v > rdy[x][y]:
-                        rdy[x][y] = v
+            for x, real in succ[k]:
+                lat = 0.0 if q == "X" or (e == "P" and eng[x] == "P") else LAT_SAME if eng[x] == e else LAT_OTHER
+                rdy[x] = max(rdy[x], end[k] + lat if real else issued)
                 left[x] -= 1
                 if left[x] == 0:
-                    ready.append(x)
-        return max(end), order, eng, start, end
+                    ready[queue[x]].append(x)
+        return max(end), order, start, end
 
-    rng = np.random.default_rng(SEED)
-    prio, bias = [MIX * base[k] - (1.0 - MIX) * k * base[0] / n for k in range(n)], [VBIAS] * n
-    best = plan(prio, bias)
-    for it in range(TRIES):
-        p2, b2 = list(prio), list(bias)
-        for _ in range(2):
-            k0 = int(rng.integers(0, n))
-            dv = float(rng.normal()) * 3.0
-            for k in range(k0, min(n, k0 + int(rng.integers(1, 12)))):
-                p2[k] += dv
-            b2[either[int(rng.integers(0, len(either)))]] = float(rng.choice([-2.0, 0.0, 1.0, 3.0]))
-        cand = plan(p2, b2)
-        if cand[0] <= best[0]:
-            best, prio, bias = cand, p2, b2
-    return best[1:]
+    def backward(end):
+        left, out = [len(s) for s in succ], [0.0] * n
+        rdy = [o["info"] + DMA_LAT if o["kind"] in "dr" and not succ[k] else 0.0 for k, o in enumerate(ops)]
+        free = {q: 0.0 for q in "VSPGYX"}
+        ready = {q: [k for k in range(n) if queue[k] == q and left[k] == 0] for q in "VSPGYX"}
+        for _ in range(n):
+            t0, q = min((max(free[q], min([rdy[k] for k in l])), q) for q, l in ready.items() if l)
+            k = max((end[k], k) for k in ready[q] if rdy[k] <= t0 + WINDOW)[1]
+            out[k] = max(rdy[k], t0) + ops[k]["alts"][eng[k]][0]
+            if q != "X":
+                free[q] = out[k]
+            ready[q].remove(k)
+            for x, real in pred[k]:
+                v = out[k] + (LAT_OTHER if real and q != "X" else 0.0)
+                if ops[x]["kind"] in "dr":
+                    v += ops[x]["info"] + ((DMA_LAT if ops[x]["kind"] == "d" else REM_LAT) if real else 0.0)
+                rdy[x] = max(rdy[x], v)
+                left[x] -= 1
+                if left[x] == 0:
+                    ready[queue[x]].append(x)
+        return [-v for v in out]
+
+    best = plan = forward(list(range(n)))
+    for _ in range(PASSES):
+        plan = forward(backward(plan[3]))
+        if plan[0] < best[0]:
+            best = plan
+    last = {}
+    for k in best[1]:
+        for b in ops[k]["banks"]:
+            for e in "VSP":
+                if e != eng[k] and (b, e) in last:
+                    ops[k]["deps"].add(last[(b, e)])
+            last[(b, eng[k])] = k
+    return best[1], eng, best[2], best[3]
 
 
 def rank_program(g, core, T, topo):
@@ -520,11 +600,15 @@ def rank_program(g, core, T, topo):
         return
     ops, Q, sent = build(g, core, T, topo)
     order, eng, start, end = schedule(ops)
+    size, sem_of = {}, {}
+    for o in ops:
+        if o["grp"] is not None:
+            size[o["grp"]] = size.get(o["grp"], 0) + 16
+            sem_of.setdefault(o["grp"], "dm%d" % len(sem_of))
     token = {}
     count = {"V": 0, "S": 0, "P": 0, "G": 0}
     seen = {}
     top = {}
-    nd = 0
     for k in order:
         o, e = ops[k], eng[k]
         if o["kind"] == "a":
@@ -533,7 +617,7 @@ def rank_program(g, core, T, topo):
         qn = "S" if e == "A" else e
         need = {}
         for d in o["deps"]:
-            if e == "P" and eng[d] == "P":
+            if (e == "P" and eng[d] == "P") or token[d] is None:
                 continue
             s, c = token[d]
             need[s] = max(need.get(s, 0), c)
@@ -542,15 +626,15 @@ def rank_program(g, core, T, topo):
                 Q[e].wait_ge(T.sem[s], need[s])
                 seen[(qn, s)] = need[s]
         ins = o["alts"][e][1]()
+        token[k] = None
         if o["kind"] == "c":
             count[e] += 1
             token[k] = ("q" + e, count[e])
             ins.then_inc(T.sem["q" + e], 1)
         elif o["kind"] == "d":
-            token[k] = ("dm%d" % nd, 16)
-            nd += 1
+            token[k] = (sem_of[o["grp"]], size[o["grp"]])
             ins.then_inc(T.sem[token[k][0]], 16)
-        if k in token:
+        if token[k] is not None:
             top[token[k][0]] = token[k][1]
     top["sent"] = sent
     for s in sorted(top, key=lambda s: (s[0] == "d", len(s), s)):

@@ -5,63 +5,65 @@ W = 4096
 RO = 3
 LW = W // 16
 GC = 1024
-LOAD = [0, 512, 1536, 2816, 4096]
+FO = W
+LOAD = [0, 1024, 2048, 3072, 4096]
 CAND = 2 * [[0, 1024, 2048, 3072, 4096]] + [[0, 1024, 2048, 3072, 3584, 4096]]
-XPATH = [{(0, 1), (2, 0), (2, 2)}] + 2 * [{(0, 0), (1, 1)}]
-CHOICE = [(0, 192), (192, 256)]
-EARLY = 1024
-TELL = 0
-LIFT = (2 * [[(1024, 2048), (2048, 3072), (3072, 4096), (0, 512), (512, 1024)]]
+XPATH = 3 * [{(0, 0), (0, 2), (0, 3)}]
+RELU = 3 * [set()]
+TELL = 1
+ZPATH = {0}
+CHOICE = [(0, 128), (128, 192), (192, 256)]
+ACROSS = {192: 0, 256: 192}
+KEYS = [[("K0", 128 * k) for k in range(3)], [("K1", 64 * k) for k in range(3)], [("K2", 128 * k) for k in range(3)]]
+LIFT = (2 * [[(0, 1024), (1024, 2048), (2048, 3072), (3072, 4096)]]
         + [[(0, 1024), (1024, 2048), (2048, 3072), (3072, 3584), (3584, 4096)]])
 MAGIC = 12582912.0
 OFF = 255.0 * 65536
 
 SCRATCH = {
-    "F0": ("sbuf", [128, 2 * W], "bfloat16"), "F1": ("sbuf", [128, 2 * W], "bfloat16"),
-    "F2": ("sbuf", [128, 2 * W], "bfloat16"), "F3": ("sbuf", [128, W], "bfloat16"),
-    "XP0": ("sbuf", [128, W + 16], "bfloat16"), "XP1": ("sbuf", [128, W + 16], "bfloat16"),
-    "XP2": ("sbuf", [128, W + 16], "bfloat16"),
-    "A": ("sbuf", [128, 3 * W], "bfloat16"), "H": ("sbuf", [128, W], "bfloat16"),
-    "Y0": ("sbuf", [128, W], "bfloat16"), "Y1": ("sbuf", [128, W], "bfloat16"), "Y2": ("sbuf", [128, W], "bfloat16"),
-    "EP": ("sbuf", [128, 4 * EARLY], "bfloat16"), "HP": ("sbuf", [128, EARLY], "bfloat16"),
-    "con": ("sbuf", [128, RO * 512], "bfloat16"), "lc": ("sbuf", [128, 512], "bfloat16"),
+    "F0": ("sbuf", [128, 2 * W + 16], "bfloat16"), "F1": ("sbuf", [128, 2 * W + 16], "bfloat16"),
+    "F2": ("sbuf", [128, 2 * W + 16], "bfloat16"), "F3": ("sbuf", [128, 2 * W], "bfloat16"),
+    "XP0": ("sbuf", [128, W], "bfloat16"), "XP1": ("sbuf", [128, W], "bfloat16"), "XP2": ("sbuf", [128, W], "bfloat16"),
+    "A": ("sbuf", [128, 3 * W], "bfloat16"), "H": ("sbuf", [128, W], "bfloat16"), "Y": ("sbuf", [128, W], "bfloat16"),
+    "con": ("sbuf", [128, RO * 512], "bfloat16"),
     "Wn": ("sbuf", [128, W], "bfloat16"), "G1": ("sbuf", [128, W], "bfloat16"), "G2": ("sbuf", [128, W], "bfloat16"),
-    "ab": ("sbuf", [128, 8, LW], "bfloat16"), "land": ("sbuf", [128, 10, LW], "bfloat16"),
-    "lu": ("sbuf", [128, 3 * LW], "uint16"), "u16": ("sbuf", [128, 9 * LW], "uint16"),
+    "ab": ("sbuf", [128, 8, LW], "bfloat16"), "land": ("sbuf", [128, 6, LW], "bfloat16"),
+    "ou": ("sbuf", [128, 7 * LW], "uint16"), "lu": ("sbuf", [128, 7 * LW], "uint16"), "u16": ("sbuf", [128, 5 * LW], "uint16"),
+    "cs": ("sbuf", [128, 8], "float32"), "cl": ("sbuf", [128, 8], "float32"),
     "qi": ("sbuf", [128, LW], "int32"), "wi": ("sbuf", [128, 2 * LW], "int32"), "abi": ("sbuf", [128, 2, LW], "int32"),
-    "lb": ("sbuf", [128, 5 * LW], "bfloat16"), "lf": ("sbuf", [128, 3 * LW], "float32"),
+    "lb": ("sbuf", [128, 3 * LW], "bfloat16"), "lf": ("sbuf", [128, 3 * LW], "float32"),
     "row": ("sbuf", [128, LW], "float32"), "blk": ("sbuf", [128, 128], "float32"), "cb": ("sbuf", [128, LW], "bfloat16"),
     "cc": ("sbuf", [128, LW], "bfloat16"), "ones": ("sbuf", [128, LW], "bfloat16"),
     "ones32": ("sbuf", [128, 128], "float32"), "I32": ("sbuf", [128, 128], "float32"),
-    "B": ("sbuf", [128, 4 * 144], "bfloat16"), "Id": ("sbuf", [128, 15 * 128], "bfloat16"),
+    "R": ("sbuf", [128, 3 * W], "bfloat16"), "B": ("sbuf", [128, 5 * 144], "bfloat16"), "Id": ("sbuf", [128, 13 * 128], "bfloat16"),
     "BB": ("sbuf", [128, 8 * 128], "bfloat16"), "Hf": ("sbuf", [128, 128], "float16"),
     "col": ("sbuf", [128, 32], "float32"), "coli": ("sbuf", [128, 16], "int32"),
-    "PKa": ("psum", [128, 512], "float32"), "PKb": ("psum", [128, 512], "float32"),
-    "PM": ("psum", [128, 512], "float32"), "PQ": ("psum", [128, 512], "float32"), "PE": ("psum", [128, 512], "float32"),
+    "K0": ("psum", [128, 512], "float32"), "K1": ("psum", [128, 512], "float32"), "K2": ("psum", [128, 512], "float32"),
+    "PM": ("psum", [128, 512], "float32"), "PE": ("psum", [128, 512], "float32"),
     "Px0": ("psum", [128, 512], "float32"), "Px1": ("psum", [128, 512], "float32"), "Px2": ("psum", [128, 512], "float32"),
 }
-SEMAPHORES = (["qV", "qS", "qP", "qG", "sent"] + ["lp%d" % i for i in range(6)] + ["fa%d" % i for i in range(24)]
-              + ["dm%d" % i for i in range(12)])
+SEMAPHORES = ["qV", "qS", "qP", "qG", "sent"] + ["fa%d" % i for i in range(40)] + ["dm%d" % i for i in range(12)]
 
 CYC, GAM, FIX, PEC = 0.00097, 1.56, 0.055, 0.00049
 LAT_OTHER, LAT_SAME = 0.1, 0.06
 DMA_LAT, DMA_RATE, REM_ISSUE, REM_FIRST, REM_LAT, REM_RATE, ROW = 1.8, 20e3, 0.6, 1.7, 1.9, 16e3, 0.02
-WINDOW, PASSES = 0.2, 2
-WHERE = {"Ga": "VSSV", "Gb": "VVVS", "DS": "S", "Z": "SSVV", "H": "VVSV", "Y": "SVSS",
-         "G1l": "SSVSV", "G1h": "SVSSV", "G1le": "SVSSS", "G1he": "SVSSS", "finl": "VSVVS", "finle": "VSSVS",
-         "HP": "S", "theirs": "VS", "G2l": "SVSS", "G2h": "VSSS", "e1": "V", "lin": "S"}
+WINDOW, TRIES, NEVER = 0.2, 2500, 1e9
+OTHER_COSTS = [(0.86, 1.0, 1.0, 1.0, 0.9), (0.86, 0.8, 1.3, 1.2, 0.9), (1.1, 1.2, 1.5, 1.3, 1.3)]
+WHERE = {"Ga": "SSSS", "Gb": "SSSS", "DS": "S", "H": "VVVV", "Y": "SSVS",
+         "G1l": "SVSV", "G1h": "SVSS", "G1le": "SVSSV", "G1he": "SVSSS", "finl": "VSVS", "finle": "VSVVS",
+         "G2l": "SSSS", "G2h": "SSSS", "e1": "S", "lin": "S"}
 
-U_M, U_POS, U_SEL, U_P1, U_E1, U_E2, U_OUT = range(7)
-(I_1, I_256, I_R16, I_16, I_N16, I_N2K, I_4K, I_8K, I_EARLY, I_2K, I_SH, I_WR, I_OFF, I_N1, I_BD) = [128 * i for i in range(15)]
-(C_P, C_PM, C_G16, C_P7, C_Q, C_LAST, C_NLAST, C_P1, C_P15, C_WC, C_WP, C_WE, C_ONE, C_CB, C_CC, C_CS, C_M0, C_M1) = range(18)
+U_M, U_POS, U_SEL, U_E1, U_E2 = range(5)
+(I_1, I_256, I_R16, I_16, I_N16, I_N2K, I_N4K, I_2K, I_SH, I_WR, I_OFF, I_N1, I_BD) = [128 * i for i in range(13)]
+(C_P, C_PM, C_G16, C_P7, C_Q, C_LAST, C_NLAST, C_P1, C_P15, C_WC, C_WE, C_ONE, C_CB, C_PW, C_CS, C_M0, C_M1) = range(17)
 C_BB, C_W0 = 18, 26
-B_KEY, B_P1, B_E1, B_CL = 0, 144, 288, 432
+B_KEY, B_E1, B_CL, B_NEG, B_TWO = [144 * i for i in range(5)]
 
 
 def build(g, core, T, topo):
     rank = T.rank_of(core)
     ops = []
-    acc = {}
+    acc, tag = {}, [0]
     Q = {"V": g.vector, "S": g.scalar, "P": g.tensor, "G": g, "Y": g.sync, "A": g.scalar}
 
     def add(name, alts, reads, writes, kind="c", extra=(), info=None):
@@ -77,12 +79,10 @@ def build(g, core, T, topo):
                 if b in SCRATCH and SCRATCH[b][0] == "psum":
                     banks.add(b)
         ops.append({"name": name, "alts": alts, "deps": deps, "kind": kind, "info": info, "banks": sorted(banks),
-                    "pick": None, "after": None, "grp": None})
+                    "pick": None, "after": None, "grp": None, "tag": tag[0]})
         return k
 
     def ap(r):
-        if r[0] in ("ab", "land") and r[2] - r[1] == 2 * LW:
-            return T[r[0]][:, r[1] // LW:r[2] // LW, :]
         if r[0] in ("ab", "abi", "land"):
             return T[r[0]][:, r[1] // LW, r[1] % LW:(r[2] - 1) % LW + 1]
         if len(r) > 3:
@@ -140,9 +140,9 @@ def build(g, core, T, topo):
         src = lambda: ap(win).indirect(ap(off))
         rd = [off] + ([win] if rows is None else rows)
         if minus is not None:
-            return add(name, {"V": (cost, lambda: g.vector.tensor_tensor(ap(o), src(), ap(minus), ALU.subtract))}, rd + [minus], [o])
+            return add(name, {"V": (cost, lambda: g.vector.tensor_tensor(ap(o), src(), ap(minus), ALU.subtract))}, rd + [minus], [o], kind="i")
         pick(add(name, {"S": (cost, lambda: g.scalar.activation(ap(o), src(), ACT.Identity, bias=0.0, scale=1.0)),
-                        "V": (cost, lambda: g.vector.tensor_copy(ap(o), src()))}, rd, [o]), name)
+                        "V": (cost, lambda: g.vector.tensor_copy(ap(o), src()))}, rd, [o], kind="i"), name)
 
     def mm(o, terms):
         def f():
@@ -175,39 +175,29 @@ def build(g, core, T, topo):
 
     sent, last, places_used, bank_turn = [0], [None], [0], [0]
 
-    def mask_of(lst):
-        return sum(1 << e for e in lst)
-
-    def send(src, dsts, nbytes, after=()):
-        def f():
-            if len(dsts) == 1:
-                c, r, s, e = dsts[0]
-                rid, pid, se = topo.addr(c)
-                return g.remote_dma(ap(r), ap(src), T.sem[s], T.sem.sent, pid, rid, mask_of(e))
-            trs = []
-            for c, r, s, e in dsts:
-                rid, pid, se = topo.addr(c)
-                trs.append(RemoteDMATransfer(dst_ids=[DstId(rid=rid, pnc=pid)], dma_engine_mask=mask_of(e),
-                                             remote_sem=T.sem[s], src=ap(src), dst=ap(r)))
-            return g.remote_dma_fused(trs, local_sem=T.sem.sent)
-        sent[0] += sum(len(d[3]) for d in dsts)
-        k = add("send", {"G": (REM_ISSUE + (REM_FIRST if last[0] is None else 0.0), f)}, [src] + list(after), [], kind="r",
-                info=(nbytes / REM_RATE + 128 * ROW) / min(len(d[3]) for d in dsts))
-        ops[k]["after"] = last[0]
-        ops[k]["to"] = (dsts, nbytes)
-        last[0] = k
-        return k
-
-    def arrive(sem, count, sends, rng):
-        return add("arr", {"X": (0.0, None)}, [], [rng], kind="a", extra=sends, info=(sem, count))
-
-    def swap(src, other, where, after=()):
+    def swap(other, parts, width=2):
         sem = "fa%d" % places_used[0]
         places_used[0] += 1
-        k = send(src, [(other, where, sem, topo.engines(core, other))], 256 * n_(src), after)
-        arrive(sem, len(topo.engines(other, core)), [k], where)
+        es = topo.engines(core, other)
+        share = len(es) // len(parts)
+        masks = [sum(1 << e for e in es[share * x:share * (x + 1)]) for x in range(len(parts))]
+
+        def f():
+            rid, pid, se = topo.addr(other)
+            if len(parts) == 1:
+                return g.remote_dma(ap(parts[0][1]), ap(parts[0][0]), T.sem[sem], T.sem.sent, pid, rid, masks[0])
+            return g.remote_dma_fused([RemoteDMATransfer(dst_ids=[DstId(rid=rid, pnc=pid)], dma_engine_mask=m, remote_sem=T.sem[sem],
+                                                         src=ap(s), dst=ap(r)) for (s, r), m in zip(parts, masks)], local_sem=T.sem.sent)
+        sent[0] += share * len(parts)
+        k = add("send", {"G": (REM_ISSUE + (REM_FIRST if last[0] is None else 0.0), f)}, [p[0] for p in parts], [], kind="r",
+                info=(128 * width * n_(parts[0][0]) / REM_RATE + 128 * ROW) / share)
+        ops[k]["after"] = last[0]
+        last[0] = k
+        count = len(topo.engines(other, core)) // len(parts) * len(parts)
+        add("arr", {"X": (0.0, None)}, [], [p[1] for p in parts], kind="a", extra=[k], info=(sem, count))
 
     partner = [T.cores[rank ^ (1 << t)] for t in range(RO)]
+    across = [T.cores[rank ^ (3 << t)] for t in range(RO - 1)]
     high = [rank > (rank ^ (1 << t)) for t in range(RO)]
 
     def col(c, n=1):
@@ -225,19 +215,28 @@ def build(g, core, T, topo):
     def lf(x, c0=0, c1=LW):
         return ("lf", x * LW + c0, x * LW + c1)
 
-    def dig(s, x, c0=0, c1=LW):
-        return ("ab", 512 * s + LW * x + c0, 512 * s + LW * x + c1)
+    def dig(s, x, c0=0, c1=LW, buf="ab"):
+        return (buf, 512 * s + LW * x + c0, 512 * s + LW * x + c1)
+
+    def theirs(t, x, c0=0, c1=LW):
+        return dig(t, x, c0, c1, "land")
+
+    def chosen(t, x, c0, c1):
+        a, b = [p for p in CHOICE if p[0] <= c0 < p[1]][0]
+        at = 512 * t + 2 * a + x * (b - a) - a
+        return ("lu", at + c0, at + c1)
 
     def px():
         bank_turn[0] += 1
         return "Px%d" % (bank_turn[0] % 3)
 
-    wrows = [("Wn%d" % r, 0, W) for r in range(6)]
+    wrows = [("Wn%d" % r, 0, W) for r in range(4)]
 
     dma(lambda: T.qi[:, :], lambda: T.ptr[:, :], [], [("qi", 0, LW)], 131072, "ptr", q="A")
     for j in range(len(LOAD) - 1):
         x0, x1 = LOAD[j], LOAD[j + 1]
-        dma(lambda x0=x0, x1=x1: T.F0[:, x0:x1], lambda x0=x0, x1=x1: T.fr[:, x0:x1], [], [("F0", x0, x1)], 256 * (x1 - x0), "fr%d" % j)
+        dma(lambda x0=x0, x1=x1: T.F0[:, FO + x0:FO + x1], lambda x0=x0, x1=x1: T.fr[:, x0:x1], [], [("F0", FO + x0, FO + x1)],
+            256 * (x1 - x0), "fr%d" % j)
     for j in range(2):
         add("ms", {"V": (vcost(W // 2, 0.5), lambda j=j: g.vector.memset(T.Wn[:, j * W // 2:(j + 1) * W // 2], 1.0))}, [],
             [(r[0], j * W // 2, (j + 1) * W // 2) for r in wrows])
@@ -252,13 +251,15 @@ def build(g, core, T, topo):
         lin(ident(c), ident(I_1), s, 0.0)
     lin(("ones", 0, LW), ("row", 0, LW), 0.0, 1.0)
     lin(col(C_Q), col(C_G16), 1.0, 15.0)
-    for c, l, wa, wb in ((C_WE, 2, 1.0, 1.0), (C_WP, 1, 256.0, 0.0625), (C_WC, 0, 1.0, 1.0)):
-        ts(col(C_W0 + l), col(C_PM), 2.0 * l, wa / 8192, ALU.is_equal, ALU.mult)
-        ts(col(c), col(C_PM), 2.0 * l + 1, wb / 8192, ALU.is_equal, ALU.mult)
+    for c, l in ((C_WE, 1), (C_WC, 0)):
+        ts(col(C_W0 + l), col(C_PM), 2.0 * l, 1.0 / 8192, ALU.is_equal, ALU.mult)
+        ts(col(c), col(C_PM), 2.0 * l + 1, 1.0 / 8192, ALU.is_equal, ALU.mult)
         lin(col(c), col(c), 1.0, col(C_W0 + l))
     ts(("B", B_KEY, B_KEY + 144), ("row", 0, 144), col(C_Q), 8192.0, ALU.is_equal, ALU.mult)
-    for b, c in ((B_E1, C_WE), (B_P1, C_WP), (B_CL, C_WC)):
+    for b, c in ((B_E1, C_WE), (B_CL, C_WC)):
         lin(("B", b, b + 144), ("B", B_KEY, B_KEY + 144), col(c), 0.0)
+    for b, s in ((B_NEG, -1.0), (B_TWO, 2.0)):
+        lin(("B", b, b + 144), ("B", B_KEY, B_KEY + 144), s, 0.0)
     ts(col(C_LAST), col(C_PM), 15.0, None, ALU.is_equal)
     lin(col(C_NLAST), col(C_LAST), -1.0, 1.0)
     lin(col(C_P1), col(C_P), 1.0, 1.0)
@@ -272,13 +273,14 @@ def build(g, core, T, topo):
 
     lin(col(C_ONE), col(C_P), 0.0, 1.0)
     set_count(col(C_ONE))
-    for c, s in ((I_N2K, -2048.0), (I_OFF, -OFF), (I_N1, -1.0), (I_4K, 4096.0), (I_2K, 2048.0)):
+    for c, s in ((I_N2K, -2048.0), (I_OFF, -OFF), (I_N1, -1.0), (I_2K, 2048.0)):
         lin(ident(c), ident(I_1), s, 0.0)
     lin(("I32", 0, 128), ident(I_1), 1.0, 0.0)
-    for c, s in ((I_16, 16.0), (I_N16, -16.0)) + (((I_8K, 8192.0),) if any(high) else ()):
+    for c, s in ((I_16, 16.0), (I_N16, -16.0)):
         lin(ident(c), ident(I_1), s, 0.0)
     if not all(high):
-        lin(ident(I_EARLY), ident(I_1), float(EARLY), 0.0)
+        lin(ident(I_N4K), ident(I_1), -4096.0, 0.0)
+        lin(col(C_PW), col(C_PM), 1.0, float(FO))
         ts(("Hf", 0, 128), ident(I_1), 0.5 - 1.0 / 2048, None, ALU.mult)
     lin(("cb", 0, LW), ("row", 0, LW), 1.0, 0.0)
     lin(("ones32", 0, 128), R128, 0.0, 1.0)
@@ -292,23 +294,11 @@ def build(g, core, T, topo):
         lin(col(C_M1), col(C_M0), -1.0, 1.0)
 
     def pad(t):
-        act(("XP%d" % t, W, W + 16), ("XP%d" % t, 0, 16), ACT.Identity)
+        act(("F%d" % t, FO + W, FO + W + 16), ("F%d" % t, FO, FO + 16), ACT.Identity)
 
-    def engines_for(src, s):
-        r = T.rank_of(src)
-        to = [T.cores[r ^ (1 << t)] for t in (s - 1, s) if 0 <= t < RO]
-        es = [topo.engines(src, c) for c in to]
-        if len(es) == 1:
-            return [es[0][-8:]]
-        only = [e for e in es[0] if e not in es[1]]
-        if only:
-            return [only, es[1]]
-        h = len(es[0]) // 2
-        return [es[0][:h], es[1][h:]]
-
-    def rows(buf, x0, l, grp):
+    def rows(buf, s, l, grp):
         for x in range(2):
-            src = (buf, x0 + LW * x, x0 + LW * x + LW)
+            src = dig(s, x, buf=buf)
             dma(lambda x=x: T.Wn[2 * l + x::16, :], lambda src=src: ap(src), [src], [wrows[2 * l + x]], 65536, grp)
 
     def digits(s, c0, c1):
@@ -318,143 +308,138 @@ def build(g, core, T, topo):
         add("cp", {"V": (vcost(2 * (c1 - c0)), lambda: g.vector.tensor_copy(T.ab[:, 2 * s:2 * s + 2, c0:c1], T.abi[:, :, c0:c1]))},
             [ai, bi], [dig(s, 0, c0, c1), dig(s, 1, c0, c1)])
 
-    def offsets(s):
-        frame = s < RO or not high[s - 1]
-        bank = "PQ" if s and frame else "PM"
-        if not s:
-            mm((bank, LW, 512), [(ident(I_256), dig(s, 0)), (ident(I_R16), dig(s, 1))])
-            cp(u16(U_OUT), (bank, LW, 512))
-        if s and not frame:
-            mm((bank, LW, 512), [(ident(I_256), dig(s, 0)), (ident(I_R16), dig(s, 1))])
-            cp(u16(U_POS), (bank, LW, 512))
-        mm(("PM", 0, LW), [(ident(I_1), dig(s, 0)), (ident(I_1), dig(s, 1))])
-        if frame:
-            cp(u16(U_M), ("PM", 0, LW))
-        if s and frame:
-            mm((bank, LW, 512), [(ident(I_256), dig(s, 0)), (ident(I_R16), dig(s, 1))])
-            cp(u16(U_POS), (bank, LW, 512))
-        if s == RO:
-            act(lf(2), ("PM", 0, LW), ACT.Identity)
-            dma(lambda: T.yp[:, :], lambda: ap(lf(2)), [lf(2)], [], 131072, "out")
+    def place_terms(s, c0, c1, at):
+        return [(ident(I_256), dig(s, 0, c0, c1), at, at + c1 - c0, 1), (ident(I_R16), dig(s, 1, c0, c1), at, at + c1 - c0, 1)]
 
-    def exchange(s):
-        ts_ = [t for t in (s - 1, s) if t < RO]
-        sl = {t: 2 * s - 2 + (t - (s - 1)) for t in ts_}
-        where = {t: ("land", 512 * sl[t], 512 * sl[t] + 512) for t in ts_}
-        es = engines_for(core, s)
-        k = send(("ab", 512 * s, 512 * s + 512), [(partner[t], where[t], "lp%d" % sl[t], es[x]) for x, t in enumerate(ts_)], 131072)
-        offsets(s)
-        if s < RO:
-            rows("ab", 512 * s, 2, "rows%d" % s)
-        for x, t in enumerate(ts_):
-            arrive("lp%d" % sl[t], len(engines_for(partner[t], s)[x]), [k], where[t])
-            rows("land", 512 * sl[t], x, "rows%d" % s)
-        join("rows%d" % s)
-
-    def second(x0, x1, end):
-        mm(("PE", x0 // 16, x1 // 16), wrap(B_E1, ("G2", x0, x1)))
-        cp(u16(U_E1, x0 // 16, x1 // 16), ("PE", x0 // 16, x1 // 16))
-        if end:
-            lin(lf(0), ("PE", 0, LW), 1.0, 4096.0 - OFF, "e1")
+    def second(t, first, name):
+        for x0 in range(0, W, GC):
+            c0, c1 = x0 // 16, (x0 + GC) // 16
+            tag[0] += 1
+            gather(("G2", x0, x0 + GC), ("G1", 0, W), (first[0], first[1] + c0, first[1] + c1), name)
+            mm(("PE", c0, c1), wrap(B_E1, ("G2", x0, x0 + GC)))
+            cp(u16(U_E1, c0, c1), ("PE", c0, c1))
+            lin(lf(0, c0, c1), ("PE", c0, c1), 1.0, 4096.0 - OFF, "e1")
 
     def before(t, c0, c1):
         terms = []
         for x in (1, 0):
-            terms.append((ident(I_SH), dig(t, x, c0, c1)))
+            terms.append((ident(I_SH), theirs(t, x, c0, c1)))
             if c0:
-                terms.append((ident(I_WR), dig(t, x, c0 - 1, c1 - 1)))
+                terms.append((ident(I_WR), theirs(t, x, c0 - 1, c1 - 1)))
             else:
-                terms.append((ident(I_WR), dig(t, x, 0, c1 - 1), 1, c1, 1))
-                terms.append((ident(I_WR), dig(t, x, LW - 1, LW), 0, 1, 1))
+                terms.append((ident(I_WR), theirs(t, x, 0, c1 - 1), 1, c1, 1))
+                terms.append((ident(I_WR), theirs(t, x, LW - 1, LW), 0, 1, 1))
         return terms
 
     def third(t):
+        count = ("cl", 4 * t - 4, 4 * t - 3) if t else col(C_ONE)
         if t:
-            set_count(col(C_CC))
-        pe = ("PE", LW, 512)
+            set_count(count)
+        pe = ("K1", LW, 512)
         mm(pe, before(t, 0, LW))
-        ts(u16(U_E2), pe, col(C_CC if t else C_ONE), None, ALU.add)
+        ts(u16(U_E2), pe, count, None, ALU.add)
         act(lb(0), pe, ACT.Sign, bias=col(C_CB))
 
+    def absdiff(a, win, off, minus, scalar, name, positive=None):
+        if positive:
+            gather(a, win, off, name, minus=minus)
+            ts(positive, a, 0.0, None, ALU.max)
+        elif scalar:
+            gather(a, win, off, "DS")
+            for p in range(0, n_(a), 512):
+                pb, piece = (px(), 0, 512), (a[0], a[1] + p, a[1] + p + 512)
+                mm(pb, [(ident(I_1), piece), (ident(I_N1), (minus[0], minus[1] + p, minus[1] + p + 512))])
+                act(piece, pb, ACT.Abs)
+        else:
+            gather(a, win, off, name, minus=minus)
+            act(a, a, ACT.Abs)
+
+    first = ("lu", 6 * LW, 7 * LW)
+    cp(("ou", 6 * LW, 7 * LW), ("qi", 0, LW))
+    swap(partner[0], [(("ou", 6 * LW, 7 * LW), first)])
     digits(0, 0, LW)
-    offsets(0)
-    rows("ab", 0, 2, "rows0")
+    swap(partner[0], [(dig(0, x), theirs(0, x)) for x in range(2)])
+    rows("land", 0, 1, "rows0")
     join("rows0")
+    mm(("PM", 0, LW), place_terms(0, 0, LW, 0))
+    cp(u16(U_POS), ("PM", 0, LW))
     for j in range(len(LOAD) - 1):
-        swap(("F0", LOAD[j], LOAD[j + 1]), partner[0], ("XP0", LOAD[j], LOAD[j + 1]))
-        if j == 0:
-            pad(0)
-            k = send(u16(U_OUT), [(partner[0], ("lu", 0, LW), "lp5", engines_for(core, 0)[0])], 65536)
-            arrive("lp5", len(engines_for(partner[0], 0)[0]), [k], ("lu", 0, LW))
+        swap(partner[0], [(("F0", FO + LOAD[j], FO + LOAD[j + 1]), ("XP0", LOAD[j], LOAD[j + 1]))])
+    pad(0)
     for x0 in range(0, W, GC):
-        gather(("G1", x0, x0 + GC), ("Wn", 0, W), ("lu", x0 // 16, (x0 + GC) // 16), "Ga", rows=wrows)
-    for x0 in range(0, W, GC):
-        gather(("G2", x0, x0 + GC), ("G1", 0, W), u16(U_M, x0 // 16, (x0 + GC) // 16), "Gb")
-        second(x0, x0 + GC, x0 + GC == W)
+        gather(("G1", x0, x0 + GC), ("Wn", 0, W), u16(U_POS, x0 // 16, (x0 + GC) // 16), "Ga", rows=wrows)
+    second(0, first, "Gb")
 
     for t in range(RO):
-        F, XP, FN, XN, Y = "F%d" % t, "XP%d" % t, "F%d" % (t + 1), "XP%d" % (t + 1), "Y%d" % t
-        win, ep = (XP, 0, W + 16), ("EP", 2 * EARLY * t, 2 * EARLY * (t + 1))
+        F, XP, FN, XN = "F%d" % t, "XP%d" % t, "F%d" % (t + 1), "XP%d" % (t + 1)
         more_rounds = t + 1 < RO
         role = "lh"[high[t]] + ("" if more_rounds else "e")
-        if more_rounds and not high[t]:
-            swap((F, 0, EARLY), partner[t + 1], (ep[0], ep[1], ep[1] + EARLY))
         third(t)
-        keys = [("PKa", 0, LW), ("PKa", LW, 512), ("PKb", 0, LW), ("PKb", LW, 512)]
-        for k in range(3):
-            for j in range(len(CAND[k]) - 1):
-                x0, x1 = CAND[k][j], CAND[k][j + 1]
-                c0, c1 = x0 // 16, x1 // 16
-                a, off = ("A", k * W + x0, k * W + x1), u16((U_M, U_E1, U_E2)[k], c0, c1)
-                if (k, j) in XPATH[t]:
-                    gather(a, win, off, "DS")
-                    for p in range(x0, x1, 512):
-                        pb, piece = (px(), 0, 512), ("A", k * W + p, k * W + p + 512)
-                        mm(pb, [(ident(I_1), piece), (ident(I_N1), (F, p, p + 512))])
-                        act(piece, pb, ACT.Abs)
-                else:
-                    gather(a, win, off, "D", minus=(F, x0, x1))
-                    act(a, a, ACT.Abs)
-                one = ("ones", 0, c1 - c0)
-                more = [[(ident(I_OFF), one), (ident(I_1), dig(t, 1, c0, c1)), (ident(I_1), dig(t, 0, c0, c1))],
-                        [(("I32", 0, 128), lf(0, c0, c1))],
-                        [(ident(I_OFF), one), (ident(I_N2K), lb(0, c0, c1)), (ident(I_2K), one),
-                         (ident(I_1), ("cc", c0, c1))] + before(t, c0, c1)][k]
-                mm((keys[k][0], keys[k][1] + c0, keys[k][1] + c1), wrap(B_KEY, a) + more)
-        k0, k1, k2, beats = keys
-        copy0, least, cleared = lf(1), ("wi", 0, LW), ("wi", LW, 2 * LW)
-        act(copy0, k0, ACT.Identity)
-        tt(least, k1, copy0, ALU.min)
-        ts(cleared, least, -4097, None, ALU.bitwise_and)
-        if high[t]:
-            tt(beats, k1, copy0, ALU.is_lt)
-        for c0, c1 in CHOICE:
-            tt(("qi", c0, c1), ("PKb", c0, c1), ("wi", LW + c0, LW + c1), ALU.min)
-            digits(t + 1, c0, c1)
-        exchange(t + 1)
-        if high[t]:
-            tt(lb(1), k2, cleared, ALU.is_lt)
-            tt(lb(2), beats, lb(1), ALU.is_gt)
-            mm(k0, [(ident(I_16), ("cb", 0, LW)), (ident(I_8K), lb(1)), (ident(I_4K), lb(2))])
-            ts(u16(U_SEL), k0, col(C_PM), None, ALU.add)
-        for x0 in range(0, W, GC):
+        for (a, b), places in zip(CHOICE, KEYS):
+            keys = [(bank, at, at + b - a) for bank, at in places]
+            for x in range(16 * a, 16 * b, GC):
+                tag[0] += 1
+                for k in range(3):
+                    for j in range(len(CAND[k]) - 1):
+                        x0, x1 = CAND[k][j], CAND[k][j + 1]
+                        if not x <= x0 < x + GC:
+                            continue
+                        c0, c1 = x0 // 16, x1 // 16
+                        d = ("A", k * W + x0, k * W + x1)
+                        off = (first[0], first[1] + c0, first[1] + c1) if k == 0 else u16((U_E1, U_E2)[k - 1], c0, c1)
+                        plus = ("R", k * W + x0, k * W + x1) if (k, j) in RELU[t] else None
+                        absdiff(d, (F, FO, FO + W + 16), off, (XP, x0, x1), (k, j) in XPATH[t], "D", plus)
+                        far = wrap(B_NEG, d) + wrap(B_TWO, plus) if plus else wrap(B_KEY, d)
+                        one = ("ones", 0, c1 - c0)
+                        more = [[(ident(I_OFF), one), (ident(I_1), theirs(t, 1, c0, c1)), (ident(I_1), theirs(t, 0, c0, c1))],
+                                [(("I32", 0, 128), lf(0, c0, c1))],
+                                [(ident(I_OFF), one), (ident(I_N2K), lb(0, c0, c1)), (ident(I_2K), one),
+                                 (ident(I_1), ("cc", c0, c1))] + before(t, c0, c1)][k]
+                        mm((keys[k][0], keys[k][1] + c0 - a, keys[k][1] + c1 - a), far + more)
+            tag[0] += 1
+            copy0, least, cleared = lf(1, a, b), ("wi", a, b), ("wi", LW + a, LW + b)
+            act(copy0, keys[0], ACT.Identity)
+            tt(least, keys[1], copy0, ALU.min)
+            ts(cleared, least, -4097, None, ALU.bitwise_and)
+            tt(("qi", a, b), keys[2], cleared, ALU.min)
+            digits(t + 1, a, b)
+            if more_rounds and b in ACROSS:
+                swap(across[t], [(dig(t + 1, x, ACROSS[b], b), theirs(t + 1, x, ACROSS[b], b)) for x in range(2)])
+            n, at = b - a, 512 * t + 2 * a
+            mm(("PM", 0, n), [(ident(I_1), dig(t + 1, 0, a, b)), (ident(I_1), dig(t + 1, 1, a, b))])
+            mm(("PM", n, 2 * n), place_terms(t + 1, a, b, 0))
+            cp(("ou", at, at + 2 * n), ("PM", 0, 2 * n))
+            swap(partner[t], [(("ou", at, at + 2 * n), ("lu", at, at + 2 * n))])
+        rows("ab", t + 1, 0, "rows%d" % (t + 1))
+        if more_rounds:
+            rows("land", t + 1, 1, "rows%d" % (t + 1))
+            first = u16(U_M)
+            mm(("PM", 0, LW), [(ident(I_1), theirs(t + 1, 0)), (ident(I_1), theirs(t + 1, 1))])
+            cp(first, ("PM", 0, LW))
+        else:
+            for a, b in CHOICE:
+                cp(lf(2, a, b), chosen(t, 0, a, b))
+            dma(lambda: T.yp[:, :], lambda: ap(lf(2)), [lf(2)], [], 131072, "out")
+        join("rows%d" % (t + 1))
+        for j, x0 in enumerate(range(0, W, GC)):
             x1 = x0 + GC
+            tag[0] += 1
+            off = chosen(t, 0, x0 // 16, x1 // 16)
             if high[t]:
-                gather((Y, x0, x1), ("A", 0, 3 * W), u16(U_SEL, x0 // 16, x1 // 16), "Z")
-                lin(("H", x0, x1), (Y, x0, x1), 0.5, -256.25, "H")
+                absdiff(("Y", x0, x1), (XP, 0, W), off, (F, FO + x0, FO + x1), j in ZPATH, "Z")
+                lin(("H", x0, x1), ("Y", x0, x1), 0.5, -256.25, "H")
             else:
-                gather((Y, x0, x1), win, u16(U_M, x0 // 16, x1 // 16), "Y")
+                gather(("Y", x0, x1), (XP, 0, W), off, "Y")
                 for p in range(x0, x1, 512):
                     pb = (px(), 0, 512)
-                    mm(pb, [(("Hf", 0, 128), (Y, p, p + 512)), (("Hf", 0, 128), (F, p, p + 512))])
-                    ts((F, W + p, W + p + 512), pb, MAGIC, -MAGIC, ALU.add, ALU.add)
-        if more_rounds:
-            swap((Y, 0, EARLY) if high[t] else (F, W, W + EARLY), partner[t + 1], (ep[0], ep[1] + EARLY, ep[2]), after=wrows)
+                    mm(pb, [(("Hf", 0, 128), ("Y", p, p + 512)), (("Hf", 0, 128), (F, FO + p, FO + p + 512))])
+                    ts((F, p, p + 512), pb, MAGIC, -MAGIC, ALU.add, ALU.add)
 
         for j, (x0, x1) in enumerate(LIFT[t]):
             c0, c1 = x0 // 16, x1 // 16
-            gather(("G1", x0, x1), ("Wn", 0, W), u16(U_POS, c0, c1), "G1" + role, rows=wrows)
-            back = ("PQ" if j & 1 else "PM", c0, c1)
+            tag[0] += 1
+            gather(("G1", x0, x1), ("Wn", 0, W), chosen(t, 1, c0, c1), "G1" + role, rows=wrows)
+            back = ("K1" if j & 1 else "K0", c0, c1)
             mm(back, wrap(B_CL, ("G1", x0, x1)) + [(ident(I_N16), ("cb", c0, c1))])
             if high[t]:
                 for b in range(2):
@@ -462,55 +447,36 @@ def build(g, core, T, topo):
             else:
                 ts(("con", 512 * t + c0, 512 * t + c1), back, col(C_PM), None, ALU.is_equal)
 
-        def smaller(out, z, h, flags, x0, x1):
-            for p in range(x0, x1, 512):
-                pb, n64 = (px(), 0, 512), (flags[0], flags[1] + p // 8, flags[1] + p // 8 + 64)
-                mm(pb, [(ident(I_1), (h, p, p + 512))] + [(("BB", 128 * i, 128 * i + 128), n64, i, 512, 8) for i in range(8)])
-                tt((out, p, p + 512), pb, (z[0], z[1] + p, z[1] + p + 512), ALU.min)
-
-        def places(out, bank, x0, x1, second_half):
-            pf = (bank, x0 // 16, x1 // 16)
-            mm(pf, [(second_half, ("con", 512 * t + x0 // 16, 512 * t + x1 // 16)), (ident(I_16), ("cb", x0 // 16, x1 // 16))])
-            ts(out, pf, col(C_PM), None, ALU.add)
-
-        mine, theirs = u16(U_OUT + 1 + t, 0, EARLY // 16), LW + LW * t
         for j, (x0, x1) in enumerate(LIFT[t]):
+            c0, c1 = x0 // 16, x1 // 16
+            tag[0] += 1
             if high[t]:
-                smaller(FN, (Y, 0), "H", ("con", 512 * t), x0, x1)
+                for p in range(x0, x1, 512):
+                    pb, n64 = (px(), 0, 512), ("con", 512 * t + p // 8, 512 * t + p // 8 + 64)
+                    mm(pb, [(ident(I_1), ("H", p, p + 512))] + [(("BB", 128 * i, 128 * i + 128), n64, i, 512, 8) for i in range(8)])
+                    tt((FN, FO + p, FO + p + 512), pb, ("Y", p, p + 512), ALU.min)
             else:
-                places(u16(U_SEL, x0 // 16, x1 // 16), "PKa", x0, x1, ident(I_4K))
-                gather((FN, x0, x1), (F, 0, 2 * W), u16(U_SEL, x0 // 16, x1 // 16), "fin" + role)
+                pf = ("K2", c0, c1)
+                mm(pf, [(ident(I_N4K), ("con", 512 * t + c0, 512 * t + c1)), (ident(I_16), ("cb", c0, c1))])
+                ts(u16(U_SEL, c0, c1), pf, col(C_PW), None, ALU.add)
+                gather((FN, FO + x0, FO + x1), (F, 0, 2 * W), u16(U_SEL, c0, c1), "fin" + role)
             if not more_rounds:
-                dma(lambda x0=x0, x1=x1: T.yf[:, x0:x1], lambda x0=x0, x1=x1: T.F3[:, x0:x1], [(FN, x0, x1)], [], 256 * (x1 - x0), "out")
+                dma(lambda x0=x0, x1=x1: T.yf[:, x0:x1], lambda x0=x0, x1=x1: T.F3[:, FO + x0:FO + x1], [(FN, FO + x0, FO + x1)], [],
+                    256 * (x1 - x0), "out")
                 continue
-            if x0 >= EARLY:
-                swap((FN, x0, x1), partner[t + 1], (XN, x0, x1))
-            if j == TELL and high[t]:
-                swap(("con", 512 * t, 512 * t + EARLY // 8), partner[t + 1], ("lc", 256 * t, 256 * t + EARLY // 8))
-            elif j == TELL:
-                places(mine, "PKb", 0, EARLY, ident(I_EARLY))
-                swap(mine, partner[t + 1], ("lu", theirs, theirs + EARLY // 16))
-            if x1 == W:
-                if high[t]:
-                    lin(("HP", 0, EARLY), (ep[0], ep[1] + EARLY, ep[2]), 0.5, -256.25, "HP")
-                    smaller(XN, (ep[0], ep[1] + EARLY), "HP", ("lc", 256 * t), 0, EARLY)
-                else:
-                    for x in (0, EARLY // 2):
-                        gather((XN, x, x + EARLY // 2), ep, ("lu", theirs + x // 16, theirs + (x + EARLY // 2) // 16), "theirs")
+            swap(partner[t + 1], [((FN, FO + x0, FO + x1), (XN, x0, x1))])
+            if j == 0:
                 pad(t + 1)
+            if j == TELL:
+                n = 2 * LW if high[t] else LW
+                act(("lb", LW, LW + n), ("con", 512 * t, 512 * t + n), ACT.Identity, accum=col(C_CS))
+                mm(("PM", 511, 512), [(("ones32", 0, 128), col(C_CS))])
+                cp(("coli", 8, 9), ("PM", 511, 512))
+                ts(("coli", 12, 13), ("coli", 8, 9), 3, None, ALU.bitwise_and)
+                ts(("cs", 4 * t, 4 * t + 1), ("coli", 12, 13), 1.0, None, ALU.add)
+                swap(partner[t + 1], [(("cs", 4 * t, 4 * t + 1), ("cl", 4 * t, 4 * t + 1))], 4)
         if more_rounds:
-            n = 2 * LW if high[t] else LW
-            act(("lb", 3 * LW, 3 * LW + n), ("con", 512 * t, 512 * t + n), ACT.Identity, accum=col(C_CS))
-            mm(("PQ", LW, LW + 1), [(("ones32", 0, 128), col(C_CS))])
-            cp(("coli", 8, 9), ("PQ", LW, LW + 1))
-            ts(("coli", 12, 13), ("coli", 8, 9), 3, None, ALU.bitwise_and)
-            ts(col(C_CC), ("coli", 12, 13), 1.0, None, ALU.add)
-            for j, x0 in enumerate(list(range(EARLY, W, GC)) + list(range(0, EARLY, GC))):
-                x1, c0, c1 = x0 + GC, x0 // 16, (x0 + GC) // 16
-                mm(("PKb", c0, c1), wrap(B_P1, ("G1", x0, x1)))
-                cp(u16(U_P1, c0, c1), ("PKb", c0, c1))
-                gather(("G2", x0, x1), ("Wn", 0, W), u16(U_P1, c0, c1), "G2" + role, rows=wrows)
-                second(x0, x1, j == W // GC - 1)
+            second(t + 1, first, "G2" + role)
     return ops, Q, sent[0]
 
 
@@ -533,9 +499,11 @@ def schedule(ops):
         free = {q: 0.0 for q in "VSPGYXM"}
         ready = {q: [k for k in range(n) if queue[k] == q and left[k] == 0] for q in "VSPGYX"}
         bank, order = {}, []
+        soonest = {q: 0.0 if l else NEVER for q, l in ready.items()}
         for _ in range(n):
-            t0, q = min((max(free[q], min([rdy[k] for k in l])), q) for q, l in ready.items() if l)
-            k = min((urge[k], k) for k in ready[q] if rdy[k] <= t0 + WINDOW)[1]
+            q = min(soonest, key=soonest.get)
+            t0 = soonest[q]
+            k = min([(urge[k], k) for k in ready[q] if rdy[k] <= t0 + WINDOW])[1]
             o, e, t = ops[k], eng[k], max(rdy[k], t0)
             for b in o["banks"]:
                 if b in bank and bank[b][1] != e:
@@ -550,12 +518,14 @@ def schedule(ops):
                 free["M"] = end[k] = max(free["M"], issued + (DMA_LAT if o["kind"] == "d" else REM_LAT)) + o["info"]
             ready[q].remove(k)
             order.append(k)
+            soonest[q] = max(free[q], min([rdy[x] for x in ready[q]])) if ready[q] else NEVER
             for x, real in succ[k]:
                 lat = 0.0 if q == "X" or (e == "P" and eng[x] == "P") else LAT_SAME if eng[x] == e else LAT_OTHER
                 rdy[x] = max(rdy[x], end[k] + lat if real else issued)
                 left[x] -= 1
                 if left[x] == 0:
                     ready[queue[x]].append(x)
+                    soonest[queue[x]] = min(soonest[queue[x]], max(free[queue[x]], rdy[x]))
         return max(end), order, start, end
 
     def backward(end):
@@ -580,11 +550,61 @@ def schedule(ops):
                     ready[queue[x]].append(x)
         return [-v for v in out]
 
-    best = plan = forward(list(range(n)))
-    for _ in range(PASSES):
-        plan = forward(backward(plan[3]))
-        if plan[0] < best[0]:
-            best = plan
+    def replay(order, fc, fg, fd, fl):
+        end, issued, bank = [0.0] * n, [0.0] * n, {}
+        free = {q: 0.0 for q in "VSPGYXM"}
+        for k in order:
+            o, e, q = ops[k], eng[k], queue[k]
+            t = free[q]
+            for d, real in pred[k]:
+                lat = 0.0 if eng[d] == "X" or (e == "P" and eng[d] == "P") else LAT_SAME if eng[d] == e else LAT_OTHER
+                t = max(t, end[d] + lat if real else issued[d])
+            for b in o["banks"]:
+                if b in bank and bank[b][1] != e:
+                    t = max(t, bank[b][0])
+            issued[k] = end[k] = t + o["alts"][e][0] * {"c": fc, "i": fc * fg, "r": fl}.get(o["kind"], 1.0)
+            if q != "X":
+                free[q] = issued[k]
+            for b in o["banks"]:
+                bank[b] = (issued[k] + LAT_OTHER, e)
+            if o["kind"] in "dr":
+                free["M"] = end[k] = max(free["M"], issued[k] + fl * (DMA_LAT if o["kind"] == "d" else REM_LAT)) + o["info"] * fd
+        return max(end)
+
+    def score(plan):
+        return plan[0] + sum(replay(plan[1], *c[:4]) / c[4] for c in OTHER_COSTS)
+
+    state = [1]
+
+    def draw(m):
+        state[0] = (state[0] * 1103515245 + 12345) % 2147483648
+        return (state[0] >> 8) % m
+
+    either = [k for k, o in enumerate(ops) if o["pick"] and o["pick"][0] != "lin"]
+    urge = backward(forward(list(range(n)))[3])
+    best = forward(urge)
+    length = score(best)
+    for _ in range(TRIES):
+        u, moved, how = list(urge), [], draw(20)
+        if how < 7:
+            moved = [either[draw(len(either))] for _ in range(1 + draw(3) // 2)]
+        elif how < 9:
+            u = backward(best[3])
+        elif how < 13:
+            which, by = ops[draw(n)]["tag"], (draw(1000) + draw(1000) - 999) / 150.0
+            u = [v + by if o["tag"] == which else v for v, o in zip(u, ops)]
+        else:
+            for _ in range(1 << draw(3)):
+                u[draw(n)] += (draw(1000) + draw(1000) - 999) / 200.0
+        for k in moved:
+            eng[k] = queue[k] = "V" if eng[k] == "S" else "S"
+        plan = forward(u)
+        new = score(plan) if plan[0] < best[0] + 1.0 else NEVER
+        if new <= length:
+            best, length, urge = plan, new, u
+        else:
+            for k in moved:
+                eng[k] = queue[k] = "V" if eng[k] == "S" else "S"
     last = {}
     for k in best[1]:
         for b in ops[k]["banks"]:
@@ -627,7 +647,7 @@ def rank_program(g, core, T, topo):
                 seen[(qn, s)] = need[s]
         ins = o["alts"][e][1]()
         token[k] = None
-        if o["kind"] == "c":
+        if o["kind"] in "ci":
             count[e] += 1
             token[k] = ("q" + e, count[e])
             ins.then_inc(T.sem["q" + e], 1)

from concourse.bass import DstId, RemoteDMATransfer
from concourse.mybir import AluOpType as ALU, ActivationFunctionType as ACT

W = 4096
RO = 3
LW = W // 16
GC = 1024
FO = W
LOAD = [0, 1024, 2048, 3072, 4096]
CAND = 2 * [[0, 1024, 2048, 3072, 4096]] + [[0, 1024, 2048, 3072, 3584, 4096]]
XPATH = 3 * [{(0, 0), (0, 2), (0, 3)}]
RELU = 3 * [set()]
TELL = 1
ZPATH = {0}
CHOICE = [(0, 128), (128, 192), (192, 256)]
ACROSS = {192: 0, 256: 192}
KEYS = [[("K0", 128 * k) for k in range(3)], [("K1", 64 * k) for k in range(3)], [("K2", 128 * k) for k in range(3)]]
LIFT = (2 * [[(0, 1024), (1024, 2048), (2048, 3072), (3072, 4096)]]
        + [[(0, 1024), (1024, 2048), (2048, 3072), (3072, 3584), (3584, 4096)]])
MAGIC = 12582912.0
OFF = 255.0 * 65536

SCRATCH = {
    "F0": ("sbuf", [128, 2 * W + 16], "bfloat16"), "F1": ("sbuf", [128, 2 * W + 16], "bfloat16"),
    "F2": ("sbuf", [128, 2 * W + 16], "bfloat16"), "F3": ("sbuf", [128, 2 * W], "bfloat16"),
    "XP0": ("sbuf", [128, W], "bfloat16"), "XP1": ("sbuf", [128, W], "bfloat16"), "XP2": ("sbuf", [128, W], "bfloat16"),
    "A": ("sbuf", [128, 3 * W], "bfloat16"), "H": ("sbuf", [128, W], "bfloat16"), "Y": ("sbuf", [128, W], "bfloat16"),
    "con": ("sbuf", [128, RO * 512], "bfloat16"),
    "Wn": ("sbuf", [128, W], "bfloat16"), "G1": ("sbuf", [128, W], "bfloat16"), "G2": ("sbuf", [128, W], "bfloat16"),
    "ab": ("sbuf", [128, 8, LW], "bfloat16"), "land": ("sbuf", [128, 6, LW], "bfloat16"),
    "ou": ("sbuf", [128, 7 * LW], "uint16"), "lu": ("sbuf", [128, 7 * LW], "uint16"), "u16": ("sbuf", [128, 5 * LW], "uint16"),
    "cs": ("sbuf", [128, 8], "float32"), "cl": ("sbuf", [128, 8], "float32"),
    "qi": ("sbuf", [128, LW], "int32"), "wi": ("sbuf", [128, 2 * LW], "int32"), "abi": ("sbuf", [128, 2, LW], "int32"),
    "lb": ("sbuf", [128, 3 * LW], "bfloat16"), "lf": ("sbuf", [128, 3 * LW], "float32"),
    "row": ("sbuf", [128, LW], "float32"), "blk": ("sbuf", [128, 128], "float32"), "cb": ("sbuf", [128, LW], "bfloat16"),
    "cc": ("sbuf", [128, LW], "bfloat16"), "ones": ("sbuf", [128, LW], "bfloat16"),
    "ones32": ("sbuf", [128, 128], "float32"), "I32": ("sbuf", [128, 128], "float32"),
    "R": ("sbuf", [128, 3 * W], "bfloat16"), "B": ("sbuf", [128, 5 * 144], "bfloat16"), "Id": ("sbuf", [128, 13 * 128], "bfloat16"),
    "BB": ("sbuf", [128, 8 * 128], "bfloat16"), "Hf": ("sbuf", [128, 128], "float16"),
    "col": ("sbuf", [128, 32], "float32"), "coli": ("sbuf", [128, 16], "int32"),
    "K0": ("psum", [128, 512], "float32"), "K1": ("psum", [128, 512], "float32"), "K2": ("psum", [128, 512], "float32"),
    "PM": ("psum", [128, 512], "float32"), "PE": ("psum", [128, 512], "float32"),
    "Px0": ("psum", [128, 512], "float32"), "Px1": ("psum", [128, 512], "float32"), "Px2": ("psum", [128, 512], "float32"),
}
SEMAPHORES = ["qV", "qS", "qP", "qG", "sent"] + ["fa%d" % i for i in range(40)] + ["dm%d" % i for i in range(12)]

CYC, GAM, FIX, PEC = 0.00097, 1.56, 0.055, 0.00049
LAT_OTHER, LAT_SAME = 0.1, 0.06
DMA_LAT, DMA_RATE, REM_ISSUE, REM_FIRST, REM_LAT, REM_RATE, ROW = 1.8, 20e3, 0.6, 1.7, 1.9, 16e3, 0.02
WINDOW, TRIES, NEVER = 0.2, 2500, 1e9
OTHER_COSTS = [(0.86, 1.0, 1.0, 1.0, 0.9), (0.86, 0.8, 1.3, 1.2, 0.9), (1.1, 1.2, 1.5, 1.3, 1.3)]
WHERE = {"Ga": "SSSS", "Gb": "SSSS", "DS": "S", "H": "VVVV", "Y": "SSVS",
         "G1l": "SVSV", "G1h": "SVSS", "G1le": "SVSSV", "G1he": "SVSSS", "finl": "VSVS", "finle": "VSVVS",
         "G2l": "SSSS", "G2h": "SSSS", "e1": "S", "lin": "S"}

U_M, U_POS, U_SEL, U_E1, U_E2 = range(5)
(I_1, I_256, I_R16, I_16, I_N16, I_N2K, I_N4K, I_2K, I_SH, I_WR, I_OFF, I_N1, I_BD) = [128 * i for i in range(13)]
(C_P, C_PM, C_G16, C_P7, C_Q, C_LAST, C_NLAST, C_P1, C_P15, C_WC, C_WE, C_ONE, C_CB, C_PW, C_CS, C_M0, C_M1) = range(17)
C_BB, C_W0 = 18, 26
B_KEY, B_E1, B_CL, B_NEG, B_TWO = [144 * i for i in range(5)]


def build(g, core, T, topo):
    rank = T.rank_of(core)
    ops = []
    acc, tag = {}, [0]
    Q = {"V": g.vector, "S": g.scalar, "P": g.tensor, "G": g, "Y": g.sync, "A": g.scalar}

    def add(name, alts, reads, writes, kind="c", extra=(), info=None):
        k = len(ops)
        deps, banks = set(extra), set()
        for lst, wr in ((reads, False), (writes, True)):
            for r in lst:
                b, lo, hi = r[:3]
                for (j, l2, h2, w2) in acc.get(b, []):
                    if j != k and (wr or w2) and l2 < hi and lo < h2:
                        deps.add(j)
                acc.setdefault(b, []).append((k, lo, hi, wr))
                if b in SCRATCH and SCRATCH[b][0] == "psum":
                    banks.add(b)
        ops.append({"name": name, "alts": alts, "deps": deps, "kind": kind, "info": info, "banks": sorted(banks),
                    "pick": None, "after": None, "grp": None, "tag": tag[0]})
        return k

    def ap(r):
        if r[0] in ("ab", "abi", "land"):
            return T[r[0]][:, r[1] // LW, r[1] % LW:(r[2] - 1) % LW + 1]
        if len(r) > 3:
            return T[r[0]][:, r[1]:r[2]:r[3]]
        return T[r[0]][:, r[1]:r[2]]

    def n_(r):
        return (r[2] - r[1] + r[3] - 1) // r[3] if len(r) > 3 else r[2] - r[1]

    def vcost(n, f=1.0):
        return FIX + max(64, n * f) * CYC

    def two(r):
        return SCRATCH[r[0]][2] in ("bfloat16", "uint16") and SCRATCH[r[0]][0] == "sbuf"

    def sc(s):
        return ap(s) if isinstance(s, tuple) else s

    def ts(o, i, s1, s2, op0, op1=None, also_s=None):
        rd = [i] + [s for s in (s1, s2) if isinstance(s, tuple)]
        if op1 is None:
            f = lambda: g.vector.tensor_scalar(ap(o), ap(i), sc(s1), None, op0)
        else:
            f = lambda: g.vector.tensor_scalar(ap(o), ap(i), sc(s1), sc(s2), op0, op1)
        alts = {"V": (vcost(n_(o), 0.5 if two(o) and two(i) else 1.0), f)}
        if also_s is not None:
            alts["S"] = (vcost(n_(o)), lambda: g.scalar.activation(ap(o), ap(i), ACT.Identity, bias=sc(also_s[1]), scale=sc(also_s[0])))
        return add("ts", alts, rd, [o])

    turn = {}

    def pick(k, name):
        turn[name] = turn.get(name, -1) + 1
        ops[k]["pick"] = (name, turn[name])

    def lin(o, i, a, b, name="lin"):
        pick(ts(o, i, a, b, ALU.mult, ALU.add, also_s=(a, b)), name)

    def cp(o, i):
        return add("cp", {"V": (vcost(n_(o), 0.5 if two(o) and two(i) else 1.0), lambda: g.vector.tensor_copy(ap(o), ap(i)))}, [i], [o])

    def tt(o, i0, i1, op):
        ps = SCRATCH[i0[0]][0] == "psum" or SCRATCH[i1[0]][0] == "psum"
        return add("tt", {"V": (vcost(n_(o), 1.0 if ps else 2.0), lambda: g.vector.tensor_tensor(ap(o), ap(i0), ap(i1), op))}, [i0, i1], [o])

    def act(o, i, func, bias=0.0, accum=None):
        rd = [i] + ([bias] if isinstance(bias, tuple) else [])
        if accum is None:
            return add("act", {"S": (vcost(n_(o)), lambda: g.scalar.activation(ap(o), ap(i), func, bias=sc(bias), scale=1.0))}, rd, [o])
        f = lambda: g.scalar.activation(ap(o), ap(i), func, bias=sc(bias), scale=1.0, accum_out=ap(accum))
        return add("act", {"S": (vcost(n_(o)), f)}, rd, [o, accum])

    def gather(o, win, off, name, minus=None, rows=None):
        cost = FIX + n_(o) * GAM * CYC
        src = lambda: ap(win).indirect(ap(off))
        rd = [off] + ([win] if rows is None else rows)
        if minus is not None:
            return add(name, {"V": (cost, lambda: g.vector.tensor_tensor(ap(o), src(), ap(minus), ALU.subtract))}, rd + [minus], [o], kind="i")
        pick(add(name, {"S": (cost, lambda: g.scalar.activation(ap(o), src(), ACT.Identity, bias=0.0, scale=1.0)),
                        "V": (cost, lambda: g.vector.tensor_copy(ap(o), src()))}, rd, [o], kind="i"), name)

    def mm(o, terms):
        def f():
            ins = None
            for x, term in enumerate(terms):
                out = T[o[0]][:, o[1] + term[2]:o[1] + term[3]:term[4]] if len(term) > 2 else ap(o)
                ins = g.tensor.matmul(out, ap(term[0]), ap(term[1]), x == 0, x == len(terms) - 1)
            return ins
        cost = FIX + sum(max(64, n_(x[1])) * PEC * (4 if SCRATCH[x[1][0]][2] == "float32" else 1) for x in terms)
        return add("mm", {"P": (cost, f)}, list({x[0] for x in terms}) + list({x[1][:3] for x in terms}), [o])

    def wrap(b0, src):
        return [(("B", b0 + 15 - i, b0 + 143 - i), (src[0], src[1] + i, src[2], 16)) for i in range(16)]

    def iota(o, pattern, cm):
        kw = {} if SCRATCH[o[0]][2] == "int32" else {"allow_small_or_imprecise_dtypes": True}
        return add("g", {"G": (0.13 + 2 * n_(o) * CYC, lambda: g.iota(ap(o), pattern, 0, cm, **kw))}, [], [o])

    groups = {}

    def dma(oap, iap, reads, writes, nbytes, grp, q="Y", rows=128):
        k = add("dma", {q: (0.1, lambda: Q[q].dma_start(oap(), iap()))}, reads, writes, kind="d",
                info=(nbytes / DMA_RATE + rows * ROW) / 16)
        ops[k]["grp"] = grp
        groups.setdefault(grp, []).append((k, writes))

    def join(grp):
        m = groups[grp]
        add("join", {"X": (0.0, None)}, [], [r for x in m for r in x[1]], kind="a", extra=[x[0] for x in m], info=None)

    sent, last, places_used, bank_turn = [0], [None], [0], [0]

    def swap(other, parts, width=2):
        sem = "fa%d" % places_used[0]
        places_used[0] += 1
        es = topo.engines(core, other)
        share = len(es) // len(parts)
        masks = [sum(1 << e for e in es[share * x:share * (x + 1)]) for x in range(len(parts))]

        def f():
            rid, pid, se = topo.addr(other)
            if len(parts) == 1:
                return g.remote_dma(ap(parts[0][1]), ap(parts[0][0]), T.sem[sem], T.sem.sent, pid, rid, masks[0])
            return g.remote_dma_fused([RemoteDMATransfer(dst_ids=[DstId(rid=rid, pnc=pid)], dma_engine_mask=m, remote_sem=T.sem[sem],
                                                         src=ap(s), dst=ap(r)) for (s, r), m in zip(parts, masks)], local_sem=T.sem.sent)
        sent[0] += share * len(parts)
        k = add("send", {"G": (REM_ISSUE + (REM_FIRST if last[0] is None else 0.0), f)}, [p[0] for p in parts], [], kind="r",
                info=(128 * width * n_(parts[0][0]) / REM_RATE + 128 * ROW) / share)
        ops[k]["after"] = last[0]
        last[0] = k
        count = len(topo.engines(other, core)) // len(parts) * len(parts)
        add("arr", {"X": (0.0, None)}, [], [p[1] for p in parts], kind="a", extra=[k], info=(sem, count))

    partner = [T.cores[rank ^ (1 << t)] for t in range(RO)]
    across = [T.cores[rank ^ (3 << t)] for t in range(RO - 1)]
    high = [rank > (rank ^ (1 << t)) for t in range(RO)]

    def col(c, n=1):
        return ("col", c, c + n)

    def ident(c):
        return ("Id", c, c + 128)

    def u16(x, c0=0, c1=LW):
        return ("u16", x * LW + c0, x * LW + c1)

    def lb(x, c0=0, c1=LW):
        return ("lb", x * LW + c0, x * LW + c1)

    def lf(x, c0=0, c1=LW):
        return ("lf", x * LW + c0, x * LW + c1)

    def dig(s, x, c0=0, c1=LW, buf="ab"):
        return (buf, 512 * s + LW * x + c0, 512 * s + LW * x + c1)

    def theirs(t, x, c0=0, c1=LW):
        return dig(t, x, c0, c1, "land")

    def chosen(t, x, c0, c1):
        a, b = [p for p in CHOICE if p[0] <= c0 < p[1]][0]
        at = 512 * t + 2 * a + x * (b - a) - a
        return ("lu", at + c0, at + c1)

    def px():
        bank_turn[0] += 1
        return "Px%d" % (bank_turn[0] % 3)

    wrows = [("Wn%d" % r, 0, W) for r in range(4)]

    dma(lambda: T.qi[:, :], lambda: T.ptr[:, :], [], [("qi", 0, LW)], 131072, "ptr", q="A")
    for j in range(len(LOAD) - 1):
        x0, x1 = LOAD[j], LOAD[j + 1]
        dma(lambda x0=x0, x1=x1: T.F0[:, FO + x0:FO + x1], lambda x0=x0, x1=x1: T.fr[:, x0:x1], [], [("F0", FO + x0, FO + x1)],
            256 * (x1 - x0), "fr%d" % j)
    for j in range(2):
        add("ms", {"V": (vcost(W // 2, 0.5), lambda j=j: g.vector.memset(T.Wn[:, j * W // 2:(j + 1) * W // 2], 1.0))}, [],
            [(r[0], j * W // 2, (j + 1) * W // 2) for r in wrows])
    iota(("coli", 0, 1), [[0, 1]], 1)
    iota(("row", 0, LW), [[1, LW]], 0)
    for x, m in ((C_P, 127), (C_PM, 15), (C_G16, 112), (C_P7, 7)):
        ts(("coli", 4 + x, 5 + x), ("coli", 0, 1), m, None, ALU.bitwise_and)
    cp(col(C_P, 4), ("coli", 4 + C_P, 8 + C_P))
    R128 = ("row", 0, 128)
    ts(ident(I_1), R128, col(C_P), None, ALU.is_equal)
    for c, s in ((I_256, 256.0), (I_R16, 0.0625)):
        lin(ident(c), ident(I_1), s, 0.0)
    lin(("ones", 0, LW), ("row", 0, LW), 0.0, 1.0)
    lin(col(C_Q), col(C_G16), 1.0, 15.0)
    for c, l in ((C_WE, 1), (C_WC, 0)):
        ts(col(C_W0 + l), col(C_PM), 2.0 * l, 1.0 / 8192, ALU.is_equal, ALU.mult)
        ts(col(c), col(C_PM), 2.0 * l + 1, 1.0 / 8192, ALU.is_equal, ALU.mult)
        lin(col(c), col(c), 1.0, col(C_W0 + l))
    ts(("B", B_KEY, B_KEY + 144), ("row", 0, 144), col(C_Q), 8192.0, ALU.is_equal, ALU.mult)
    for b, c in ((B_E1, C_WE), (B_CL, C_WC)):
        lin(("B", b, b + 144), ("B", B_KEY, B_KEY + 144), col(c), 0.0)
    for b, s in ((B_NEG, -1.0), (B_TWO, 2.0)):
        lin(("B", b, b + 144), ("B", B_KEY, B_KEY + 144), s, 0.0)
    ts(col(C_LAST), col(C_PM), 15.0, None, ALU.is_equal)
    lin(col(C_NLAST), col(C_LAST), -1.0, 1.0)
    lin(col(C_P1), col(C_P), 1.0, 1.0)
    lin(col(C_P15), col(C_P), 1.0, -15.0)
    for c, a, b in ((I_SH, C_P1, C_NLAST), (I_WR, C_P15, C_LAST)):
        ts(ident(c), R128, col(a), col(b), ALU.is_equal, ALU.mult)

    def set_count(c):
        lin(col(C_CB), c, 1.0, -4095.5)
        lin(("cc", 0, LW), ("ones", 0, LW), c, 0.0)

    lin(col(C_ONE), col(C_P), 0.0, 1.0)
    set_count(col(C_ONE))
    for c, s in ((I_N2K, -2048.0), (I_OFF, -OFF), (I_N1, -1.0), (I_2K, 2048.0)):
        lin(ident(c), ident(I_1), s, 0.0)
    lin(("I32", 0, 128), ident(I_1), 1.0, 0.0)
    for c, s in ((I_16, 16.0), (I_N16, -16.0)):
        lin(ident(c), ident(I_1), s, 0.0)
    if not all(high):
        lin(ident(I_N4K), ident(I_1), -4096.0, 0.0)
        lin(col(C_PW), col(C_PM), 1.0, float(FO))
        ts(("Hf", 0, 128), ident(I_1), 0.5 - 1.0 / 2048, None, ALU.mult)
    lin(("cb", 0, LW), ("row", 0, LW), 1.0, 0.0)
    lin(("ones32", 0, 128), R128, 0.0, 1.0)
    if any(high):
        iota(("blk", 0, 128), [[16, 8], [0, 16]], 0)
        ts(ident(I_BD), ("blk", 0, 128), col(C_G16), None, ALU.is_equal)
        ts(col(C_BB, 8), ("row", 0, 8), col(C_P7), 256.0, ALU.is_equal, ALU.mult)
        for i in range(8):
            lin(("BB", 128 * i, 128 * i + 128), ident(I_BD), col(C_BB + i), 0.0)
        ts(col(C_M0), col(C_PM), 8.0, None, ALU.is_ge)
        lin(col(C_M1), col(C_M0), -1.0, 1.0)

    def pad(t):
        act(("F%d" % t, FO + W, FO + W + 16), ("F%d" % t, FO, FO + 16), ACT.Identity)

    def rows(buf, s, l, grp):
        for x in range(2):
            src = dig(s, x, buf=buf)
            dma(lambda x=x: T.Wn[2 * l + x::16, :], lambda src=src: ap(src), [src], [wrows[2 * l + x]], 65536, grp)

    def digits(s, c0, c1):
        ai, bi = ("abi", c0, c1), ("abi", LW + c0, LW + c1)
        ts(ai, ("qi", c0, c1), 15, None, ALU.bitwise_and)
        ts(bi, ("qi", c0, c1), 4080, None, ALU.bitwise_and)
        add("cp", {"V": (vcost(2 * (c1 - c0)), lambda: g.vector.tensor_copy(T.ab[:, 2 * s:2 * s + 2, c0:c1], T.abi[:, :, c0:c1]))},
            [ai, bi], [dig(s, 0, c0, c1), dig(s, 1, c0, c1)])

    def place_terms(s, c0, c1, at):
        return [(ident(I_256), dig(s, 0, c0, c1), at, at + c1 - c0, 1), (ident(I_R16), dig(s, 1, c0, c1), at, at + c1 - c0, 1)]

    def second(t, first, name):
        for x0 in range(0, W, GC):
            c0, c1 = x0 // 16, (x0 + GC) // 16
            tag[0] += 1
            gather(("G2", x0, x0 + GC), ("G1", 0, W), (first[0], first[1] + c0, first[1] + c1), name)
            mm(("PE", c0, c1), wrap(B_E1, ("G2", x0, x0 + GC)))
            cp(u16(U_E1, c0, c1), ("PE", c0, c1))
            lin(lf(0, c0, c1), ("PE", c0, c1), 1.0, 4096.0 - OFF, "e1")

    def before(t, c0, c1):
        terms = []
        for x in (1, 0):
            terms.append((ident(I_SH), theirs(t, x, c0, c1)))
            if c0:
                terms.append((ident(I_WR), theirs(t, x, c0 - 1, c1 - 1)))
            else:
                terms.append((ident(I_WR), theirs(t, x, 0, c1 - 1), 1, c1, 1))
                terms.append((ident(I_WR), theirs(t, x, LW - 1, LW), 0, 1, 1))
        return terms

    def third(t):
        count = ("cl", 4 * t - 4, 4 * t - 3) if t else col(C_ONE)
        if t:
            set_count(count)
        pe = ("K1", LW, 512)
        mm(pe, before(t, 0, LW))
        ts(u16(U_E2), pe, count, None, ALU.add)
        act(lb(0), pe, ACT.Sign, bias=col(C_CB))

    def absdiff(a, win, off, minus, scalar, name, positive=None):
        if positive:
            gather(a, win, off, name, minus=minus)
            ts(positive, a, 0.0, None, ALU.max)
        elif scalar:
            gather(a, win, off, "DS")
            for p in range(0, n_(a), 512):
                pb, piece = (px(), 0, 512), (a[0], a[1] + p, a[1] + p + 512)
                mm(pb, [(ident(I_1), piece), (ident(I_N1), (minus[0], minus[1] + p, minus[1] + p + 512))])
                act(piece, pb, ACT.Abs)
        else:
            gather(a, win, off, name, minus=minus)
            act(a, a, ACT.Abs)

    first = ("lu", 6 * LW, 7 * LW)
    cp(("ou", 6 * LW, 7 * LW), ("qi", 0, LW))
    swap(partner[0], [(("ou", 6 * LW, 7 * LW), first)])
    digits(0, 0, LW)
    swap(partner[0], [(dig(0, x), theirs(0, x)) for x in range(2)])
    rows("land", 0, 1, "rows0")
    join("rows0")
    mm(("PM", 0, LW), place_terms(0, 0, LW, 0))
    cp(u16(U_POS), ("PM", 0, LW))
    for j in range(len(LOAD) - 1):
        swap(partner[0], [(("F0", FO + LOAD[j], FO + LOAD[j + 1]), ("XP0", LOAD[j], LOAD[j + 1]))])
    pad(0)
    for x0 in range(0, W, GC):
        gather(("G1", x0, x0 + GC), ("Wn", 0, W), u16(U_POS, x0 // 16, (x0 + GC) // 16), "Ga", rows=wrows)
    second(0, first, "Gb")

    for t in range(RO):
        F, XP, FN, XN = "F%d" % t, "XP%d" % t, "F%d" % (t + 1), "XP%d" % (t + 1)
        more_rounds = t + 1 < RO
        role = "lh"[high[t]] + ("" if more_rounds else "e")
        third(t)
        for (a, b), places in zip(CHOICE, KEYS):
            keys = [(bank, at, at + b - a) for bank, at in places]
            for x in range(16 * a, 16 * b, GC):
                tag[0] += 1
                for k in range(3):
                    for j in range(len(CAND[k]) - 1):
                        x0, x1 = CAND[k][j], CAND[k][j + 1]
                        if not x <= x0 < x + GC:
                            continue
                        c0, c1 = x0 // 16, x1 // 16
                        d = ("A", k * W + x0, k * W + x1)
                        off = (first[0], first[1] + c0, first[1] + c1) if k == 0 else u16((U_E1, U_E2)[k - 1], c0, c1)
                        plus = ("R", k * W + x0, k * W + x1) if (k, j) in RELU[t] else None
                        absdiff(d, (F, FO, FO + W + 16), off, (XP, x0, x1), (k, j) in XPATH[t], "D", plus)
                        far = wrap(B_NEG, d) + wrap(B_TWO, plus) if plus else wrap(B_KEY, d)
                        one = ("ones", 0, c1 - c0)
                        more = [[(ident(I_OFF), one), (ident(I_1), theirs(t, 1, c0, c1)), (ident(I_1), theirs(t, 0, c0, c1))],
                                [(("I32", 0, 128), lf(0, c0, c1))],
                                [(ident(I_OFF), one), (ident(I_N2K), lb(0, c0, c1)), (ident(I_2K), one),
                                 (ident(I_1), ("cc", c0, c1))] + before(t, c0, c1)][k]
                        mm((keys[k][0], keys[k][1] + c0 - a, keys[k][1] + c1 - a), far + more)
            tag[0] += 1
            copy0, least, cleared = lf(1, a, b), ("wi", a, b), ("wi", LW + a, LW + b)
            act(copy0, keys[0], ACT.Identity)
            tt(least, keys[1], copy0, ALU.min)
            ts(cleared, least, -4097, None, ALU.bitwise_and)
            tt(("qi", a, b), keys[2], cleared, ALU.min)
            digits(t + 1, a, b)
            if more_rounds and b in ACROSS:
                swap(across[t], [(dig(t + 1, x, ACROSS[b], b), theirs(t + 1, x, ACROSS[b], b)) for x in range(2)])
            n, at = b - a, 512 * t + 2 * a
            mm(("PM", 0, n), [(ident(I_1), dig(t + 1, 0, a, b)), (ident(I_1), dig(t + 1, 1, a, b))])
            mm(("PM", n, 2 * n), place_terms(t + 1, a, b, 0))
            cp(("ou", at, at + 2 * n), ("PM", 0, 2 * n))
            swap(partner[t], [(("ou", at, at + 2 * n), ("lu", at, at + 2 * n))])
        rows("ab", t + 1, 0, "rows%d" % (t + 1))
        if more_rounds:
            rows("land", t + 1, 1, "rows%d" % (t + 1))
            first = u16(U_M)
            mm(("PM", 0, LW), [(ident(I_1), theirs(t + 1, 0)), (ident(I_1), theirs(t + 1, 1))])
            cp(first, ("PM", 0, LW))
        else:
            for a, b in CHOICE:
                cp(lf(2, a, b), chosen(t, 0, a, b))
            dma(lambda: T.yp[:, :], lambda: ap(lf(2)), [lf(2)], [], 131072, "out")
        join("rows%d" % (t + 1))
        for j, x0 in enumerate(range(0, W, GC)):
            x1 = x0 + GC
            tag[0] += 1
            off = chosen(t, 0, x0 // 16, x1 // 16)
            if high[t]:
                absdiff(("Y", x0, x1), (XP, 0, W), off, (F, FO + x0, FO + x1), j in ZPATH, "Z")
                lin(("H", x0, x1), ("Y", x0, x1), 0.5, -256.25, "H")
            else:
                gather(("Y", x0, x1), (XP, 0, W), off, "Y")
                for p in range(x0, x1, 512):
                    pb = (px(), 0, 512)
                    mm(pb, [(("Hf", 0, 128), ("Y", p, p + 512)), (("Hf", 0, 128), (F, FO + p, FO + p + 512))])
                    ts((F, p, p + 512), pb, MAGIC, -MAGIC, ALU.add, ALU.add)

        for j, (x0, x1) in enumerate(LIFT[t]):
            c0, c1 = x0 // 16, x1 // 16
            tag[0] += 1
            gather(("G1", x0, x1), ("Wn", 0, W), chosen(t, 1, c0, c1), "G1" + role, rows=wrows)
            back = ("K1" if j & 1 else "K0", c0, c1)
            mm(back, wrap(B_CL, ("G1", x0, x1)) + [(ident(I_N16), ("cb", c0, c1))])
            if high[t]:
                for b in range(2):
                    ts(("con", 512 * t + 2 * c0 + b, 512 * t + 2 * c1, 2), back, col(C_PM), col(C_M0 + b), ALU.is_equal, ALU.max)
            else:
                ts(("con", 512 * t + c0, 512 * t + c1), back, col(C_PM), None, ALU.is_equal)

        for j, (x0, x1) in enumerate(LIFT[t]):
            c0, c1 = x0 // 16, x1 // 16
            tag[0] += 1
            if high[t]:
                for p in range(x0, x1, 512):
                    pb, n64 = (px(), 0, 512), ("con", 512 * t + p // 8, 512 * t + p // 8 + 64)
                    mm(pb, [(ident(I_1), ("H", p, p + 512))] + [(("BB", 128 * i, 128 * i + 128), n64, i, 512, 8) for i in range(8)])
                    tt((FN, FO + p, FO + p + 512), pb, ("Y", p, p + 512), ALU.min)
            else:
                pf = ("K2", c0, c1)
                mm(pf, [(ident(I_N4K), ("con", 512 * t + c0, 512 * t + c1)), (ident(I_16), ("cb", c0, c1))])
                ts(u16(U_SEL, c0, c1), pf, col(C_PW), None, ALU.add)
                gather((FN, FO + x0, FO + x1), (F, 0, 2 * W), u16(U_SEL, c0, c1), "fin" + role)
            if not more_rounds:
                dma(lambda x0=x0, x1=x1: T.yf[:, x0:x1], lambda x0=x0, x1=x1: T.F3[:, FO + x0:FO + x1], [(FN, FO + x0, FO + x1)], [],
                    256 * (x1 - x0), "out")
                continue
            swap(partner[t + 1], [((FN, FO + x0, FO + x1), (XN, x0, x1))])
            if j == 0:
                pad(t + 1)
            if j == TELL:
                n = 2 * LW if high[t] else LW
                act(("lb", LW, LW + n), ("con", 512 * t, 512 * t + n), ACT.Identity, accum=col(C_CS))
                mm(("PM", 511, 512), [(("ones32", 0, 128), col(C_CS))])
                cp(("coli", 8, 9), ("PM", 511, 512))
                ts(("coli", 12, 13), ("coli", 8, 9), 3, None, ALU.bitwise_and)
                ts(("cs", 4 * t, 4 * t + 1), ("coli", 12, 13), 1.0, None, ALU.add)
                swap(partner[t + 1], [(("cs", 4 * t, 4 * t + 1), ("cl", 4 * t, 4 * t + 1))], 4)
        if more_rounds:
            second(t + 1, first, "G2" + role)
    return ops, Q, sent[0]


def schedule(ops):
    n = len(ops)
    eng = [WHERE[o["pick"][0]][o["pick"][1] % len(WHERE[o["pick"][0]])] if o["pick"] else list(o["alts"])[0] for o in ops]
    queue = ["S" if e == "A" else e for e in eng]
    succ, pred, above = [[] for _ in range(n)], [[] for _ in range(n)], []
    for k, o in enumerate(ops):
        implied = set()
        for d in o["deps"]:
            implied |= above[d]
        above.append(implied | o["deps"])
        for d in sorted((o["deps"] - implied) | ({o["after"]} - {None})):
            succ[d].append((k, d in o["deps"]))
            pred[k].append((d, d in o["deps"]))

    def forward(urge):
        left, rdy, start, end = [len(p) for p in pred], [0.0] * n, [0.0] * n, [0.0] * n
        free = {q: 0.0 for q in "VSPGYXM"}
        ready = {q: [k for k in range(n) if queue[k] == q and left[k] == 0] for q in "VSPGYX"}
        bank, order = {}, []
        soonest = {q: 0.0 if l else NEVER for q, l in ready.items()}
        for _ in range(n):
            q = min(soonest, key=soonest.get)
            t0 = soonest[q]
            k = min([(urge[k], k) for k in ready[q] if rdy[k] <= t0 + WINDOW])[1]
            o, e, t = ops[k], eng[k], max(rdy[k], t0)
            for b in o["banks"]:
                if b in bank and bank[b][1] != e:
                    t = max(t, bank[b][0])
            start[k], issued = t, t + o["alts"][e][0]
            end[k] = issued
            if q != "X":
                free[q] = issued
            for b in o["banks"]:
                bank[b] = (issued + LAT_OTHER, e)
            if o["kind"] in "dr":
                free["M"] = end[k] = max(free["M"], issued + (DMA_LAT if o["kind"] == "d" else REM_LAT)) + o["info"]
            ready[q].remove(k)
            order.append(k)
            soonest[q] = max(free[q], min([rdy[x] for x in ready[q]])) if ready[q] else NEVER
            for x, real in succ[k]:
                lat = 0.0 if q == "X" or (e == "P" and eng[x] == "P") else LAT_SAME if eng[x] == e else LAT_OTHER
                rdy[x] = max(rdy[x], end[k] + lat if real else issued)
                left[x] -= 1
                if left[x] == 0:
                    ready[queue[x]].append(x)
                    soonest[queue[x]] = min(soonest[queue[x]], max(free[queue[x]], rdy[x]))
        return max(end), order, start, end

    def backward(end):
        left, out = [len(s) for s in succ], [0.0] * n
        rdy = [o["info"] + DMA_LAT if o["kind"] in "dr" and not succ[k] else 0.0 for k, o in enumerate(ops)]
        free = {q: 0.0 for q in "VSPGYX"}
        ready = {q: [k for k in range(n) if queue[k] == q and left[k] == 0] for q in "VSPGYX"}
        for _ in range(n):
            t0, q = min((max(free[q], min([rdy[k] for k in l])), q) for q, l in ready.items() if l)
            k = max((end[k], k) for k in ready[q] if rdy[k] <= t0 + WINDOW)[1]
            out[k] = max(rdy[k], t0) + ops[k]["alts"][eng[k]][0]
            if q != "X":
                free[q] = out[k]
            ready[q].remove(k)
            for x, real in pred[k]:
                v = out[k] + (LAT_OTHER if real and q != "X" else 0.0)
                if ops[x]["kind"] in "dr":
                    v += ops[x]["info"] + ((DMA_LAT if ops[x]["kind"] == "d" else REM_LAT) if real else 0.0)
                rdy[x] = max(rdy[x], v)
                left[x] -= 1
                if left[x] == 0:
                    ready[queue[x]].append(x)
        return [-v for v in out]

    def replay(order, fc, fg, fd, fl):
        end, issued, bank = [0.0] * n, [0.0] * n, {}
        free = {q: 0.0 for q in "VSPGYXM"}
        for k in order:
            o, e, q = ops[k], eng[k], queue[k]
            t = free[q]
            for d, real in pred[k]:
                lat = 0.0 if eng[d] == "X" or (e == "P" and eng[d] == "P") else LAT_SAME if eng[d] == e else LAT_OTHER
                t = max(t, end[d] + lat if real else issued[d])
            for b in o["banks"]:
                if b in bank and bank[b][1] != e:
                    t = max(t, bank[b][0])
            issued[k] = end[k] = t + o["alts"][e][0] * {"c": fc, "i": fc * fg, "r": fl}.get(o["kind"], 1.0)
            if q != "X":
                free[q] = issued[k]
            for b in o["banks"]:
                bank[b] = (issued[k] + LAT_OTHER, e)
            if o["kind"] in "dr":
                free["M"] = end[k] = max(free["M"], issued[k] + fl * (DMA_LAT if o["kind"] == "d" else REM_LAT)) + o["info"] * fd
        return max(end)

    def score(plan):
        return plan[0] + sum(replay(plan[1], *c[:4]) / c[4] for c in OTHER_COSTS)

    state = [1]

    def draw(m):
        state[0] = (state[0] * 1103515245 + 12345) % 2147483648
        return (state[0] >> 8) % m

    either = [k for k, o in enumerate(ops) if o["pick"] and o["pick"][0] != "lin"]
    urge = backward(forward(list(range(n)))[3])
    best = forward(urge)
    length = score(best)
    for _ in range(TRIES):
        u, moved, how = list(urge), [], draw(20)
        if how < 7:
            moved = [either[draw(len(either))] for _ in range(1 + draw(3) // 2)]
        elif how < 9:
            u = backward(best[3])
        elif how < 13:
            which, by = ops[draw(n)]["tag"], (draw(1000) + draw(1000) - 999) / 150.0
            u = [v + by if o["tag"] == which else v for v, o in zip(u, ops)]
        else:
            for _ in range(1 << draw(3)):
                u[draw(n)] += (draw(1000) + draw(1000) - 999) / 200.0
        for k in moved:
            eng[k] = queue[k] = "V" if eng[k] == "S" else "S"
        plan = forward(u)
        new = score(plan) if plan[0] < best[0] + 1.0 else NEVER
        if new <= length:
            best, length, urge = plan, new, u
        else:
            for k in moved:
                eng[k] = queue[k] = "V" if eng[k] == "S" else "S"
    last = {}
    for k in best[1]:
        for b in ops[k]["banks"]:
            for e in "VSP":
                if e != eng[k] and (b, e) in last:
                    ops[k]["deps"].add(last[(b, e)])
            last[(b, eng[k])] = k
    return best[1], eng, best[2], best[3]


def rank_program(g, core, T, topo):
    if T.rank_of(core) is None:
        return
    ops, Q, sent = build(g, core, T, topo)
    order, eng, start, end = schedule(ops)
    size, sem_of = {}, {}
    for o in ops:
        if o["grp"] is not None:
            size[o["grp"]] = size.get(o["grp"], 0) + 16
            sem_of.setdefault(o["grp"], "dm%d" % len(sem_of))
    token = {}
    count = {"V": 0, "S": 0, "P": 0, "G": 0}
    seen = {}
    top = {}
    for k in order:
        o, e = ops[k], eng[k]
        if o["kind"] == "a":
            token[k] = o["info"]
            continue
        qn = "S" if e == "A" else e
        need = {}
        for d in o["deps"]:
            if (e == "P" and eng[d] == "P") or token[d] is None:
                continue
            s, c = token[d]
            need[s] = max(need.get(s, 0), c)
        for s in sorted(need):
            if seen.get((qn, s), 0) < need[s]:
                Q[e].wait_ge(T.sem[s], need[s])
                seen[(qn, s)] = need[s]
        ins = o["alts"][e][1]()
        token[k] = None
        if o["kind"] in "ci":
            count[e] += 1
            token[k] = ("q" + e, count[e])
            ins.then_inc(T.sem["q" + e], 1)
        elif o["kind"] == "d":
            token[k] = (sem_of[o["grp"]], size[o["grp"]])
            ins.then_inc(T.sem[token[k][0]], 16)
        if token[k] is not None:
            top[token[k][0]] = token[k][1]
    top["sent"] = sent
    for s in sorted(top, key=lambda s: (s[0] == "d", len(s), s)):
        if max([v for (qn, s2), v in seen.items() if s2 == s] + [0]) < top[s]:
            g.wait_ge(T.sem[s], top[s])
